import numpy as np
import ml_dtypes


def mxq(x, axis, fmt="e4m3"):
    dtype, down = {"e4m3": (ml_dtypes.float8_e4m3fn, 7), "e5m2": (ml_dtypes.float8_e5m2, 14)}[fmt]
    v = np.moveaxis(np.asarray(x, np.float32).astype(ml_dtypes.bfloat16).astype(np.float64), axis, -1)
    blocks = v.reshape(v.shape[:-1] + (-1, 32))
    amax = np.abs(blocks).max(-1, keepdims=True)
    byte = np.maximum(np.where(amax > 0, np.frexp(amax)[1] - 1 + 127, 0) - down, 1)
    scale = np.exp2(byte - 127.0)
    codes = (blocks / scale).astype(np.float32).astype(dtype).astype(np.float64)
    return np.moveaxis((codes * scale).reshape(v.shape), -1, axis)


WIDE = False


def mx_kscale(k):
    if not WIDE:
        return np.ones(k)
    levels = np.array([10, -10, 5, -5, 0])
    if k % 512:
        return np.exp2(np.random.permutation(np.resize(levels, k // 32))).repeat(32)
    a = np.empty((k // 512, 16))
    for p in range(k // 512):
        a[p, :8] = np.random.permutation(np.resize(levels, 8))
        for g in range(8):
            far = levels[np.abs(levels - a[p, g]) >= 10]
            a[p, g + 8] = far[np.random.randint(len(far))]
    return np.exp2(a.ravel()).repeat(32)


BF16 = ml_dtypes.bfloat16


def bf(x):
    return np.asarray(x, np.float32).astype(BF16)


def f64(x):
    return np.asarray(x).astype(np.float64)


E2M1 = np.array([0.0, 0.5, 1.0, 1.5, 2.0, 3.0, 4.0, 6.0, -0.0, -0.5, -1.0, -1.5, -2.0, -3.0, -4.0, -6.0])


def pack_weight(w, fmt):
    k, n = w.shape
    w = f64(bf(w)).reshape(k // 32, 32, n)
    amax = np.abs(w).max(1)
    if fmt == "e4m3":
        byte = np.frexp(amax)[1] - 1 + 127 - 7
    else:
        mant, ex = np.frexp(amax / 6.0)
        byte = np.where(mant > 0.5, ex, ex - 1) + 127
    byte = np.clip(np.where(amax > 0, byte, 1), 1, 254)
    scaled = (w * np.exp2(127.0 - byte)[:, None, :]).reshape(k, n).astype(np.float32)
    by_word = np.ascontiguousarray(scaled.reshape(k // 512, 128, 4, n).transpose(0, 1, 3, 2))
    if fmt == "e4m3":
        words = by_word.astype(ml_dtypes.float8_e4m3fn).view(np.uint8)
    else:
        c = by_word.astype(ml_dtypes.float4_e2m1fn).view(np.uint8) & 0xF
        words = c[..., 0::2] | (c[..., 1::2] << 4)
    return np.ascontiguousarray(words), np.ascontiguousarray(byte.astype(np.uint8).reshape(k // 512, 16, n))


def unpack_weight(words, scales, fmt):
    g, p, n, _ = words.shape
    if fmt == "e4m3":
        vals = np.ascontiguousarray(words).view(ml_dtypes.float8_e4m3fn).astype(np.float64)
    else:
        nib = np.empty((g, p, n, 4), np.uint8)
        nib[..., 0::2] = words & 0xF
        nib[..., 1::2] = words >> 4
        vals = E2M1[nib]
    vals = vals * np.repeat(np.exp2(scales.astype(np.float64) - 127.0), 8, axis=1)[..., None]
    return vals.transpose(0, 1, 3, 2).reshape(g * 512, n)
def pack4(w):
    words, scales = pack_weight(w, "e2m1")
    return words.reshape(words.shape[0], 128, -1), scales


def unpack4(words, scales):
    return unpack_weight(words.reshape(words.shape[0], 128, -1, 2), scales, "e2m1")


def planes(Y):
    n, m = Y.shape
    b = f64(bf(Y)).reshape(n // 32, 32, m)
    amax = np.abs(b).max(1)
    byte = np.clip(np.where(amax > 0, np.frexp(amax)[1] - 1 + 127 - 7, 1), 1, 254)
    codes = (b * np.exp2(127.0 - byte)[:, None, :]).reshape(n, m).astype(np.float32).astype(ml_dtypes.float8_e4m3fn).view(np.uint8)
    words = codes.reshape(n // 512, 128, 4, m).transpose(0, 1, 3, 2)
    return np.ascontiguousarray(words), np.ascontiguousarray(byte.astype(np.uint8).reshape(n // 512, 16, m))


B, S, Z, R = 2048, 1024, 512, 1024


def setup_inputs():
    s, u, t = mx_kscale(S), mx_kscale(Z), mx_kscale(R)
    rn = np.random.randn
    log_x = bf(rn(B, S) * s)
    log_z = bf(rn(B, Z) * u)
    f_words, f_scales = pack4(0.5 * rn(S, R) / np.sqrt(S) / s[:, None])
    e_orders = bf(0.5 * rn(Z, R) / np.sqrt(Z) / u[:, None])
    rate_const = bf(np.exp(0.4 * rn(R)) * t)
    p_words, p_scales = pack_weight(rn(R, S) / np.sqrt(R) / t[:, None], "e4m3")
    inflow = bf(0.5 * rn(B, S))
    unit = bf(np.exp(0.8 * rn(S)))
    return {"log_x": log_x, "log_z": log_z, "f_words": f_words, "f_scales": f_scales,
            "e_orders": e_orders, "rate_const": rate_const, "p_words": p_words,
            "p_scales": p_scales, "inflow": inflow, "unit": unit}


def reference(log_x, log_z, f_words, f_scales, e_orders, rate_const, p_words, p_scales, inflow, unit):
    F = unpack4(f_words, f_scales)
    P = unpack_weight(p_words, p_scales, "e4m3")
    a = mxq(f64(log_x), 1, "e4m3") @ F
    a = a + (mxq(f64(log_z), 1, "e4m3") @ mxq(f64(e_orders), 0, "e4m3"))
    v = np.exp(a) * f64(rate_const)
    y = ((mxq(v, 1, "e4m3") @ P) + f64(inflow)) * f64(unit)
    Y = y.T
    words, scales = planes(Y)
    return y, words, scales

@@ -1,0 +1,444 @@
+from contextlib import ExitStack
+
+import concourse.mybir as mybir
+from concourse.masks import make_identity
+
+B, S, Z, R = 2048, 1024, 512, 1024
+FLOPS = 2 * B * (S * R + Z * R + R * S)
+
+F32 = mybir.dt.float32
+BF16 = mybir.dt.bfloat16
+U32 = mybir.dt.uint32
+I32 = mybir.dt.int32
+U8 = mybir.dt.uint8
+FP8X4 = mybir.dt.float8_e4m3fn_x4
+FP4X4 = mybir.dt.float4_e2m1fn_x4
+ALU = mybir.AluOpType
+ACT = mybir.ActivationFunctionType
+
+P = 128
+TILES = B // P
+CHUNKS = [(0, 4), (4, 8), (8, 12), (12, 16)]
+IN_UNITS = [(0, 2), (2, 4), (4, 6), (6, 8), (8, 10), (10, 12), (12, 14), (14, 16)]
+OUT_UNITS = [(0, 2), (2, 4), (4, 6), (6, 8), (8, 10), (10, 12), (12, 14), (14, 15), (15, 16)]
+IN_LEAD = 5
+GCOLS = 640
+RATE_PSUM = False
+PS_BUFS = 7
+E_ON_V = (0, 1)
+YCOPY_V = ()
+CLAG = 5
+DLAG = 2
+XB = 8
+UNIT_PSUM = True
+TAILJ = 11
+GTAIL = 512
+IN_AT = {4: 1, 5: 2, 6: 4, 7: 6}
+S2FIRST = 13
+SPLIT = False
+GRP = 8
+IN_TICK = [-2, -1, 0, 1, 2, 3, 5, 7]
+S1_PER = [2, 2, 2, 2]
+RATE0 = 2
+YB = 4
+
+
+def tile_power_law_net_production_k6_kernel(
+    tc, log_x, log_z, f_words, f_scales, e_orders, rate_const, p_words, p_scales, inflow, unit, out_0, out_1, out_2
+):
+    nc = tc.nc
+    with ExitStack() as ctx:
+        keep = ctx.enter_context(tc.tile_pool(name="keep", bufs=1))
+        work = ctx.enter_context(tc.tile_pool(name="work", bufs=2))
+        psum = ctx.enter_context(tc.psum_pool(name="psum", bufs=1))
+        ctx.enter_context(tc.manual_schedule())
+
+        def kept(name, shape, dtype):
+            return keep.tile(shape, dtype, name=name, align_bytes=64)
+
+        def staged(tag, shape, dtype, bufs):
+            return work.tile(shape, dtype, name=tag, tag=tag, bufs=bufs, align_bytes=64)
+
+        def bank():
+            return psum.tile([P, 512], F32, name="bank", tag="bank", bufs=PS_BUFS)
+
+        ident = kept("ident", [P, P], F32)
+        make_identity(nc, ident[:])
+        rows = kept("rows", [P, 512], BF16)
+        nc.vector.memset(rows[:], 0.0)
+        fs_raw = kept("fs_raw", [P, 2, R], U8)
+        p_sc = kept("p_sc", [P, 2, S], U8)
+        nc.vector.memset(fs_raw[:].rearrange("p g n -> p (g n)").bitcast(I32), 0)
+        nc.vector.memset(p_sc[:].rearrange("p g n -> p (g n)").bitcast(I32), 0)
+        warm = kept("warm", [P, 16], F32)
+        nc.vector.memset(warm[:, 0:8], 0.0)
+        nc.scalar.activation(out=warm[:, 8:16], in_=warm[:, 0:8], func=ACT.Exp)
+
+        x_codes = [kept("x_codes%d" % g, [P, B], U32) for g in range(3)]
+        x_sc = [kept("x_sc%d" % g, [P, B], U8) for g in range(3)]
+        v_codes = [kept("v_codes%d" % h, [P, B], U32) for h in range(2)]
+        v_sc = [kept("v_sc%d" % h, [P, B], U8) for h in range(2)]
+        y_codes = kept("y_codes", [P, 2, B], U32)
+        y_sc = kept("y_sc", [P, 2, B], U8)
+
+        x_raw, z_raw, flow, y_f32, y_bf, expo = {}, {}, {}, {}, {}, {}
+
+        def load_x(j):
+            x_raw[j] = staged("x_raw", [P, S], BF16, XB)
+            nc.sync.dma_start(out=x_raw[j][:], in_=log_x[j * P : (j + 1) * P, :])
+
+        def load_z(j):
+            pair = staged("z_raw", [P, 2, Z], BF16, XB // 2)
+            nc.sync.dma_start(out=pair[:], in_=log_z[j * P : (j + 2) * P, :].rearrange("(i p) k -> p i k", i=2))
+            z_raw[j], z_raw[j + 1] = pair[:, 0, :], pair[:, 1, :]
+
+        def load_in(j):
+            load_x(j)
+            load_x(j + 1)
+            load_z(j)
+
+        def load_flow(j):
+            flow[j] = staged("flow", [P, S], BF16, 5)
+            nc.sync.dma_start(out=flow[j][:], in_=inflow[j * P : (j + 1) * P, :])
+
+        def load_scales(plane, rows):
+            for q in range(4):
+                nc.sync.dma_start(
+                    out=plane[32 * q : 32 * q + 4, :, :].bitcast(I32),
+                    in_=rows[:, 4 * q : 4 * q + 4, :].rearrange("g r n -> r g n").bitcast(I32),
+                )
+
+        f_raw, e_raw, f_codes, f_sc, e_grp, e_codes, e_sc = {}, {}, {}, {}, {}, {}, {}
+
+        def load_f(h):
+            f_raw[h] = kept("f_raw%d" % h, [P, 2, 1024], U8)
+            nc.sync.dma_start(
+                out=f_raw[h][:].bitcast(I32),
+                in_=f_words[:, :, 1024 * h : 1024 * (h + 1)].rearrange("g p b -> p g b").bitcast(I32),
+            )
+
+        def load_e(h):
+            e_raw[h] = staged("y_f32", [P, 4, 512], BF16, YB)
+            nc.sync.dma_start(
+                out=e_raw[h][:], in_=e_orders[:, 512 * h : 512 * (h + 1)].rearrange("(p j) c -> p j c", j=4)
+            )
+
+        def sort_f(h):
+            f_codes[h] = kept("f_codes%d" % h, [P, 2, 1024], U8)
+            nc.vector.tensor_copy(
+                out=f_codes[h][:].rearrange("p g (t m b) -> p g t m b", t=4, b=2),
+                in_=f_raw[h][:].rearrange("p g (m t b) -> p g t m b", t=4, b=2),
+            )
+
+        def sort_fs(h):
+            f_sc[h] = kept("f_sc%d" % h, [P, 2, 512], U8)
+            nc.vector.tensor_copy(
+                out=f_sc[h][:].rearrange("p g (t m) -> p g t m", t=4),
+                in_=fs_raw[:, :, 512 * h : 512 * (h + 1)].rearrange("p g (m t) -> p g t m", t=4),
+            )
+
+        def sort_e(h):
+            e_grp[h] = staged("y_f32", [P, 2048], BF16, YB)
+            dst = e_grp[h][:].rearrange("p (t a b j) -> p a t b j", t=4, b=2, j=4)
+            src = e_raw[h][:].rearrange("p j (a b t) -> p a t b j", b=2, t=4)
+            if h in E_ON_V:
+                nc.vector.tensor_copy(out=dst, in_=src)
+            else:
+                nc.scalar.copy(out=dst, in_=src)
+
+        def quant_e(h):
+            e_codes[h] = kept("e_codes%d" % h, [P, 512], U32)
+            e_sc[h] = kept("e_sc%d" % h, [P, 512], U8)
+            nc.vector.quantize_mx(out=e_codes[h][:].bitcast(FP8X4), scales=e_sc[h][:], in_=e_grp[h][:])
+
+        def turn(words_of, tiles, step, on_vector):
+            n = len(tiles)
+            ps = bank()
+            for i, j in enumerate(tiles):
+                for u in range(2):
+                    nc.tensor.transpose(ps[:, (2 * i + u) * P : (2 * i + u + 1) * P], words_of(j, u), ident[:])
+            grp = staged("grp", [P, 1024], BF16, GRP)
+            dst = grp[:, : n * 512].bitcast(F32).rearrange("p (i c u) -> p i c u", i=n, u=2)
+            src = ps[:, : n * 256].rearrange("p (i u c) -> p i c u", i=n, u=2)
+            if on_vector:
+                nc.vector.tensor_copy(out=dst, in_=src)
+            else:
+                nc.scalar.copy(out=dst, in_=src)
+            return grp
+
+        def quant(grp, codes, scales, a, b):
+            nc.vector.quantize_mx(
+                out=codes[:, a * P : b * P].bitcast(FP8X4), scales=scales[:, a * P : b * P], in_=grp[:, : (b - a) * 512]
+            )
+
+        def turn_in(a, b, g):
+            src = x_raw if g < 2 else z_raw
+            k0 = 256 * (g % 2)
+            grp = turn(lambda j, u: src[j][:].bitcast(F32)[:, k0 + u : k0 + 256 : 2], range(a, b), 2, False)
+            return lambda: quant(grp, x_codes[g], x_sc[g], a, b)
+
+        def turn_out(a, b, g, on_v=False):
+            grp = turn(
+                lambda j, u: y_bf[j][:].bitcast(F32)[:, (2 * g + u) * P : (2 * g + u + 1) * P], range(a, b), 1, on_v
+            )
+            return lambda: quant(grp, y_codes[:, g, :], y_sc[:, g, :], a, b)
+
+        def log_rate_passes(out, h, t, a, b):
+            cells = slice(a * P, b * P)
+            for g in range(3):
+                if g < 2:
+                    w = f_codes[h][:, g, 256 * t : 256 * (t + 1)].bitcast(FP4X4)
+                    ws = f_sc[h][:, g, P * t : P * (t + 1)]
+                else:
+                    w = e_codes[h][:, P * t : P * (t + 1)].bitcast(FP8X4)
+                    ws = e_sc[h][:, P * t : P * (t + 1)]
+                nc.tensor.matmul_mx(
+                    out=out, lhsT=w, lhsT_scale=ws, rhs=x_codes[g][:, cells].bitcast(FP8X4), rhs_scale=x_sc[g][:, cells],
+                    start=(g == 0), stop=(g == 2),
+                )
+
+        def stage1_wide(a, b, h, t):
+            if t == 0:
+                expo[a, h] = staged("expo", [P, 4, 512], F32, 3)
+            ps = bank()
+            log_rate_passes(ps[:], h, t, a, b)
+            nc.scalar.activation(out=expo[a, h][:, t, :], in_=ps[:], func=ACT.Exp)
+
+        def stage1_narrow(a, h):
+            expo[a, h] = staged("expo_n", [P, 1, 512], F32, 4)
+            ps = bank()
+            for t in range(4):
+                log_rate_passes(ps[:, t * P : (t + 1) * P], h, t, a, a + 1)
+            nc.scalar.activation(
+                out=expo[a, h][:, 0, :].rearrange("p (c t) -> p c t", t=4),
+                in_=ps[:].rearrange("p (t c) -> p c t", t=4), func=ACT.Exp,
+            )
+
+        def rates(chunk, h, a, b):
+            grp = staged("grp", [P, 1024], BF16, GRP)
+            n = (b - a) * P
+            if chunk[1] - chunk[0] == 1:
+                nc.vector.tensor_tensor(
+                    out=grp[:, :512].rearrange("p (c t) -> p c t", t=4),
+                    in0=expo[a, h][:, 0, :].rearrange("p (c t) -> p c t", t=4),
+                    in1=rate_of(h).unsqueeze(1).to_broadcast([P, P, 4]), op=ALU.mult,
+                )
+            else:
+                c0 = (a - chunk[0]) * P
+                nc.vector.tensor_tensor(
+                    out=grp[:, : 4 * n].rearrange("p (c i t) -> p c t i", i=2, t=4),
+                    in0=expo[chunk[0], h][:, :, c0 : c0 + n].rearrange("p t (c i) -> p c t i", i=2),
+                    in1=rate_of(h).unsqueeze(1).unsqueeze(3).to_broadcast([P, n // 2, 4, 2]), op=ALU.mult,
+                )
+            return lambda: quant(grp, v_codes[h], v_sc[h], a, b)
+
+        def gcols(j):
+            return GCOLS if j < TAILJ else GTAIL
+
+        def stage2(j):
+            y_f32[j] = staged("y_f32", [P, S], F32, YB)
+            cells = slice(j * P, (j + 1) * P)
+            for n in range(2):
+                cols = slice(512 * n, 512 * (n + 1))
+                ps = bank()
+                for h in range(2):
+                    nc.tensor.matmul_mx(
+                        out=ps[:], lhsT=v_codes[h][:, cells].bitcast(FP8X4), lhsT_scale=v_sc[h][:, cells],
+                        rhs=p_codes[:, h, cols].bitcast(FP8X4), rhs_scale=p_sc[:, h, cols], start=(h == 0), stop=(h == 1),
+                    )
+                nc.vector.tensor_tensor(out=y_f32[j][:, cols], in0=ps[:], in1=flow[j][:, cols], op=ALU.add)
+                lo, hi = 512 * n, min(512 * (n + 1), gcols(j))
+                if hi > lo:
+                    nc.gpsimd.tensor_tensor(out=y_f32[j][:, lo:hi], in0=y_f32[j][:, lo:hi], in1=unit_bc[:, lo:hi], op=ALU.mult)
+
+        def to_mass(j):
+            c = gcols(j)
+            if c < S:
+                nc.vector.tensor_tensor(out=y_f32[j][:, c:], in0=y_f32[j][:, c:], in1=unit_hi[:, c - 512 :], op=ALU.mult)
+
+        def round_y(j):
+            nc.sync.dma_start(out=out_0[j * P : (j + 1) * P, :], in_=y_f32[j][:])
+            y_bf[j] = staged("y_bf", [P, S], BF16, 4)
+            nc.scalar.copy(
+                out=y_bf[j][:].rearrange("p (g u q e) -> p g u q e", g=2, u=2, e=2),
+                in_=y_f32[j][:].rearrange("p (g q u e) -> p g u q e", g=2, u=2, e=2),
+            )
+
+        def round_half(j, g, copy):
+            cols = slice(512 * g, 512 * (g + 1))
+            nc.sync.dma_start(out=out_0[j * P : (j + 1) * P, cols], in_=y_f32[j][:, cols])
+            copy(
+                out=y_bf[j][:, cols].rearrange("p (u q e) -> p u q e", u=2, e=2),
+                in_=y_f32[j][:, cols].rearrange("p (q u e) -> p u q e", u=2, e=2),
+            )
+
+        def store_codes(a, b):
+            nc.sync.dma_start(
+                out=out_1[:, :, a * P : b * P, :].rearrange("g p m t -> p g (m t)").bitcast(I32),
+                in_=y_codes[:, :, a * P : b * P].bitcast(I32),
+            )
+
+        def store_scales(a, b):
+            for q in range(4):
+                nc.sync.dma_start(
+                    out=out_2[:, 4 * q : 4 * q + 4, a * P : b * P].rearrange("g r m -> r g m").bitcast(I32),
+                    in_=y_sc[32 * q : 32 * q + 4, :, a * P : b * P].bitcast(I32),
+                )
+
+        ident_bf = kept("ident_bf", [P, P], BF16)
+        nc.vector.tensor_copy(out=ident_bf[:], in_=ident[:])
+        load_f(0)
+        nc.sync.dma_start(out=rows[0:2, :], in_=rate_const.rearrange("(h n) -> h n", h=2))
+        nc.sync.dma_start(out=rows[2:4, :], in_=unit.rearrange("(h n) -> h n", h=2))
+        load_scales(fs_raw, f_scales)
+        load_e(0)
+        load_in(0)
+        load_in(2)
+        load_f(1)
+        load_e(1)
+        load_in(4)
+        load_in(6)
+        p_codes = kept("p_codes", [P, 2, S], U32)
+        nc.sync.dma_start(out=p_codes[:].bitcast(I32), in_=p_words.rearrange("g p n t -> p g (n t)").bitcast(I32))
+        load_scales(p_sc, p_scales)
+        load_flow(0)
+        load_flow(1)
+
+        def turn_in_unit(a):
+            return [turn_in(a, a + 2, g) for g in range(3)]
+
+        def run(todos):
+            for todo in todos:
+                todo()
+
+        consts = psum.tile([P, 1024], BF16, name="consts", tag="consts")
+        for t in range(4):
+            nc.tensor.transpose(consts[:, t * P : (t + 1) * P], rows[:, t:512:4], ident_bf[:])
+        rate_of = lambda h: consts[:, :512].rearrange("p (t r) -> p t r", t=4)[:, :, h]
+        unit_hi = consts[:, 512:]
+        ps = bank()
+        cols_ps = ps[:].bitcast(BF16)
+        for c in range(4):
+            nc.tensor.transpose(cols_ps[:, c * P : (c + 1) * P], rows[:, c * P : (c + 1) * P], ident_bf[:])
+        unit_col = kept("unit_col", [P, 4, 2], BF16)
+        nc.scalar.copy(out=unit_col[:], in_=cols_ps[:, :512].rearrange("p (c r) -> p c r", c=4)[:, :, 2:4])
+        ps = bank()
+        unit_ps = ps[:].bitcast(BF16)
+        for c in range(8):
+            nc.tensor.transpose(
+                unit_ps[:, c * P : (c + 1) * P], unit_col[:, c % 4, c // 4 : c // 4 + 1].to_broadcast([P, P]), ident_bf[:]
+            )
+        for c in range(4):
+            nc.tensor.transpose(unit_hi[:, c * P : (c + 1) * P], unit_col[:, c, 1:2].to_broadcast([P, P]), ident_bf[:])
+        unit_bc = kept("unit_bc", [P, S], BF16)
+        nc.scalar.copy(out=unit_bc[:], in_=unit_ps)
+
+        c0 = CHUNKS[0]
+        sort_f(0)
+        sort_fs(0)
+        sort_e(0)
+        q0 = turn_in_unit(0)
+        quant_e(0)
+        run(q0)
+        run(turn_in_unit(2))
+        sort_f(1)
+        sort_fs(1)
+        for t in range(4):
+            stage1_wide(0, 4, 0, t)
+        sort_e(1)
+        q2 = turn_in_unit(4)
+        quant_e(1)
+        qv = rates(c0, 0, 0, 2)
+        stage1_wide(0, 4, 1, 0)
+        stage1_wide(0, 4, 1, 1)
+        run(q2)
+        qv()
+        qv = rates(c0, 0, 2, 4)
+        q3 = turn_in_unit(6)
+        stage1_wide(0, 4, 1, 2)
+        stage1_wide(0, 4, 1, 3)
+        run(q3)
+        qv()
+
+        in_at, s1_at, rate_at, out_at = {}, {}, {}, {}
+        for u, k in IN_AT.items():
+            in_at.setdefault(k, []).extend([(2 * u, 0), (2 * u, 1), (2 * u, 2)])
+        for a, b in CHUNKS:
+            for i in range(8):
+                if a > 0:
+                    s1_at.setdefault(a - 5 + i // 2, []).append((a, b, i // 4, i % 4))
+            for i in range(4):
+                lo = a + 2 * (i % 2)
+                if a > 0 or i > 1:
+                    rate_at.setdefault(a - 3 + i, []).append(((a, b), i // 2, lo, lo + 2))
+        for a, b in OUT_UNITS:
+            out_at.setdefault(b - 1 + DLAG, []).append((a, b))
+
+        pending = []
+        for k in range(-1, 11):
+            for a, g in in_at.get(k + 2, []):
+                if g == 0 and a >= 8:
+                    load_in(a)
+            if 2 <= k + 3 < TILES:
+                load_flow(k + 3)
+            run(pending)
+            late = []
+            for a, g in in_at.get(k, []):
+                late.append(turn_in(a, a + 2, g))
+            for a, b in out_at.get(k, []):
+                for g in range(2):
+                    late.append(turn_out(a, b, g))
+                if b % 4 == 0:
+                    late.append(lambda b=b: store_codes(b - 4, b))
+            if 0 <= k - 1:
+                round_y(k - 1)
+            if 0 <= k:
+                stage2(k)
+            for chunk, h, a, b in rate_at.get(k, []):
+                late.insert(1, rates(chunk, h, a, b))
+            if 0 <= k:
+                to_mass(k)
+            for a, b, h, t in s1_at.get(k, []):
+                stage1_wide(a, b, h, t)
+            pending = late
+
+        last = CHUNKS[-1]
+        load_flow(14)
+        run(pending)
+        qy = [turn_out(8, 10, g) for g in range(2)]
+        qv = rates(last, 1, 12, 14)
+        round_y(10)
+        load_flow(15)
+        run([qy[0], qv, qy[1]])
+        stage2(11)
+        to_mass(11)
+        round_y(11)
+        stage2(12)
+        qv = rates(last, 1, 14, 16)
+        to_mass(12)
+        qv()
+        stage2(13)
+        qy = [turn_out(10, 12, g) for g in range(2)]
+        round_y(12)
+        to_mass(13)
+        round_y(13)
+        stage2(14)
+        to_mass(14)
+        run(qy)
+        store_codes(8, 12)
+        store_scales(0, 12)
+        stage2(15)
+        qy = [turn_out(12, 14, g) for g in range(2)]
+        round_y(14)
+        to_mass(15)
+        run(qy)
+        qy = [turn_out(14, 15, g) for g in range(2)]
+        y_bf[15] = staged("y_bf", [P, S], BF16, 4)
+        round_half(15, 1, nc.scalar.copy)
+        round_half(15, 0, nc.vector.tensor_copy)
+        run(qy)
+        store_codes(12, 15)
+        qy = [turn_out(15, 16, 1), turn_out(15, 16, 0, True)]
+        run(qy)
+        store_codes(15, 16)
+        store_scales(12, 16)

@@ -22,14 +22,16 @@ CHUNKS = [(0, 4), (4, 8), (8, 12), (12, 16)]
 IN_UNITS = [(0, 2), (2, 4), (4, 6), (6, 8), (8, 10), (10, 12), (12, 14), (14, 16)]
 OUT_UNITS = [(0, 2), (2, 4), (4, 6), (6, 8), (8, 10), (10, 12), (12, 14), (14, 15), (15, 16)]
 IN_LEAD = 5
-GCOLS = 640
+GCOLS = 704
 RATE_PSUM = False
-PS_BUFS = 7
-E_ON_V = (0, 1)
+MM_BUFS = 4
+E_ON_V = (0,)
 YCOPY_V = ()
 CLAG = 5
 DLAG = 2
 XB = 8
+LASTG = 2
+SC_FIRST = True
 UNIT_PSUM = True
 TAILJ = 11
 GTAIL = 512
@@ -40,7 +42,7 @@ GRP = 8
 IN_TICK = [-2, -1, 0, 1, 2, 3, 5, 7]
 S1_PER = [2, 2, 2, 2]
 RATE0 = 2
-YB = 4
+YB = 5
 
 
 def tile_power_law_net_production_k6_kernel(
@@ -59,8 +61,8 @@ def tile_power_law_net_production_k6_kernel(
         def staged(tag, shape, dtype, bufs):
             return work.tile(shape, dtype, name=tag, tag=tag, bufs=bufs, align_bytes=64)
 
-        def bank():
-            return psum.tile([P, 512], F32, name="bank", tag="bank", bufs=PS_BUFS)
+        def bank(tag="mm"):
+            return psum.tile([P, 512], F32, name=tag, tag=tag, bufs=MM_BUFS if tag == "mm" else 7 - MM_BUFS)
 
         ident = kept("ident", [P, P], F32)
         make_identity(nc, ident[:])
@@ -83,14 +85,24 @@ def tile_power_law_net_production_k6_kernel(
 
         x_raw, z_raw, flow, y_f32, y_bf, expo = {}, {}, {}, {}, {}, {}
 
+        k_rows = {}
+
+        def load_first(g):
+            src = log_x[:512, 512 * g : 512 * (g + 1)] if g < 2 else log_z[:512, :]
+            four = kept("first%d" % g, [P, 4, 512], BF16)
+            nc.sync.dma_start(out=four[:], in_=src.rearrange("(i p) k -> p i k", i=4))
+            for j in range(4):
+                k_rows[j, g] = four[:, j, :]
+
         def load_x(j):
             x_raw[j] = staged("x_raw", [P, S], BF16, XB)
             nc.sync.dma_start(out=x_raw[j][:], in_=log_x[j * P : (j + 1) * P, :])
+            k_rows[j, 0], k_rows[j, 1] = x_raw[j][:, :512], x_raw[j][:, 512:]
 
         def load_z(j):
             pair = staged("z_raw", [P, 2, Z], BF16, XB // 2)
             nc.sync.dma_start(out=pair[:], in_=log_z[j * P : (j + 2) * P, :].rearrange("(i p) k -> p i k", i=2))
-            z_raw[j], z_raw[j + 1] = pair[:, 0, :], pair[:, 1, :]
+            k_rows[j, 2], k_rows[j + 1, 2] = pair[:, 0, :], pair[:, 1, :]
 
         def load_in(j):
             load_x(j)
@@ -153,7 +165,7 @@ def tile_power_law_net_production_k6_kernel(
 
         def turn(words_of, tiles, step, on_vector):
             n = len(tiles)
-            ps = bank()
+            ps = bank("tp")
             for i, j in enumerate(tiles):
                 for u in range(2):
                     nc.tensor.transpose(ps[:, (2 * i + u) * P : (2 * i + u + 1) * P], words_of(j, u), ident[:])
@@ -172,9 +184,7 @@ def tile_power_law_net_production_k6_kernel(
             )
 
         def turn_in(a, b, g):
-            src = x_raw if g < 2 else z_raw
-            k0 = 256 * (g % 2)
-            grp = turn(lambda j, u: src[j][:].bitcast(F32)[:, k0 + u : k0 + 256 : 2], range(a, b), 2, False)
+            grp = turn(lambda j, u: k_rows[j, g].bitcast(F32)[:, u:256:2], range(a, b), 2, False)
             return lambda: quant(grp, x_codes[g], x_sc[g], a, b)
 
         def turn_out(a, b, g, on_v=False):
@@ -183,9 +193,9 @@ def tile_power_law_net_production_k6_kernel(
             )
             return lambda: quant(grp, y_codes[:, g, :], y_sc[:, g, :], a, b)
 
-        def log_rate_passes(out, h, t, a, b):
+        def log_rate_passes(out, h, t, a, b, gs=(0, 1, 2)):
             cells = slice(a * P, b * P)
-            for g in range(3):
+            for g in gs:
                 if g < 2:
                     w = f_codes[h][:, g, 256 * t : 256 * (t + 1)].bitcast(FP4X4)
                     ws = f_sc[h][:, g, P * t : P * (t + 1)]
@@ -194,7 +204,7 @@ def tile_power_law_net_production_k6_kernel(
                     ws = e_sc[h][:, P * t : P * (t + 1)]
                 nc.tensor.matmul_mx(
                     out=out, lhsT=w, lhsT_scale=ws, rhs=x_codes[g][:, cells].bitcast(FP8X4), rhs_scale=x_sc[g][:, cells],
-                    start=(g == 0), stop=(g == 2),
+                    start=(g == 0), stop=(g == LASTG),
                 )
 
         def stage1_wide(a, b, h, t):
@@ -235,10 +245,11 @@ def tile_power_law_net_production_k6_kernel(
         def gcols(j):
             return GCOLS if j < TAILJ else GTAIL
 
-        def stage2(j):
-            y_f32[j] = staged("y_f32", [P, S], F32, YB)
+        def stage2(j, halves=(0, 1)):
+            if 0 in halves:
+                y_f32[j] = staged("y_f32", [P, S], F32, YB)
             cells = slice(j * P, (j + 1) * P)
-            for n in range(2):
+            for n in halves:
                 cols = slice(512 * n, 512 * (n + 1))
                 ps = bank()
                 for h in range(2):
@@ -272,8 +283,8 @@ def tile_power_law_net_production_k6_kernel(
                 in_=y_f32[j][:, cols].rearrange("p (q u e) -> p u q e", u=2, e=2),
             )
 
-        def store_codes(a, b):
-            nc.sync.dma_start(
+        def store_codes(a, b, queue=nc.sync):
+            queue.dma_start(
                 out=out_1[:, :, a * P : b * P, :].rearrange("g p m t -> p g (m t)").bitcast(I32),
                 in_=y_codes[:, :, a * P : b * P].bitcast(I32),
             )
@@ -287,13 +298,14 @@ def tile_power_law_net_production_k6_kernel(
 
         ident_bf = kept("ident_bf", [P, P], BF16)
         nc.vector.tensor_copy(out=ident_bf[:], in_=ident[:])
+        load_first(0)
         load_f(0)
+        load_first(1)
+        load_scales(fs_raw, f_scales)
         nc.sync.dma_start(out=rows[0:2, :], in_=rate_const.rearrange("(h n) -> h n", h=2))
         nc.sync.dma_start(out=rows[2:4, :], in_=unit.rearrange("(h n) -> h n", h=2))
-        load_scales(fs_raw, f_scales)
+        load_first(2)
         load_e(0)
-        load_in(0)
-        load_in(2)
         load_f(1)
         load_e(1)
         load_in(4)
@@ -312,42 +324,60 @@ def tile_power_law_net_production_k6_kernel(
                 todo()
 
         consts = psum.tile([P, 1024], BF16, name="consts", tag="consts")
-        for t in range(4):
-            nc.tensor.transpose(consts[:, t * P : (t + 1) * P], rows[:, t:512:4], ident_bf[:])
         rate_of = lambda h: consts[:, :512].rearrange("p (t r) -> p t r", t=4)[:, :, h]
         unit_hi = consts[:, 512:]
-        ps = bank()
-        cols_ps = ps[:].bitcast(BF16)
-        for c in range(4):
-            nc.tensor.transpose(cols_ps[:, c * P : (c + 1) * P], rows[:, c * P : (c + 1) * P], ident_bf[:])
         unit_col = kept("unit_col", [P, 4, 2], BF16)
-        nc.scalar.copy(out=unit_col[:], in_=cols_ps[:, :512].rearrange("p (c r) -> p c r", c=4)[:, :, 2:4])
-        ps = bank()
-        unit_ps = ps[:].bitcast(BF16)
-        for c in range(8):
-            nc.tensor.transpose(
-                unit_ps[:, c * P : (c + 1) * P], unit_col[:, c % 4, c // 4 : c // 4 + 1].to_broadcast([P, P]), ident_bf[:]
-            )
-        for c in range(4):
-            nc.tensor.transpose(unit_hi[:, c * P : (c + 1) * P], unit_col[:, c, 1:2].to_broadcast([P, P]), ident_bf[:])
         unit_bc = kept("unit_bc", [P, S], BF16)
-        nc.scalar.copy(out=unit_bc[:], in_=unit_ps)
+
+        def consts_down():
+            for t in range(4):
+                nc.tensor.transpose(consts[:, t * P : (t + 1) * P], rows[:, t:512:4], ident_bf[:])
+            ps = bank("tp")
+            cols_ps = ps[:].bitcast(BF16)
+            for c in range(4):
+                nc.tensor.transpose(cols_ps[:, c * P : (c + 1) * P], rows[:, c * P : (c + 1) * P], ident_bf[:])
+            nc.scalar.copy(out=unit_col[:], in_=cols_ps[:, :512].rearrange("p (c r) -> p c r", c=4)[:, :, 2:4])
+
+        def consts_across():
+            ps = bank("tp")
+            unit_ps = ps[:].bitcast(BF16)
+            for c in range(8):
+                nc.tensor.transpose(
+                    unit_ps[:, c * P : (c + 1) * P], unit_col[:, c % 4, c // 4 : c // 4 + 1].to_broadcast([P, P]), ident_bf[:]
+                )
+            for c in range(4):
+                nc.tensor.transpose(unit_hi[:, c * P : (c + 1) * P], unit_col[:, c, 1:2].to_broadcast([P, P]), ident_bf[:])
+            nc.scalar.copy(out=unit_bc[:], in_=unit_ps)
+
+        def first_passes(banks, g, ts):
+            for t in ts:
+                log_rate_passes(banks[t][:], 0, t, 0, 4, (g,))
 
         c0 = CHUNKS[0]
+        qx = [turn_in(0, 2, 0), turn_in(2, 4, 0)]
         sort_f(0)
+        run(qx)
+        qx = [turn_in(0, 2, 1), turn_in(2, 4, 1)]
         sort_fs(0)
-        sort_e(0)
-        q0 = turn_in_unit(0)
-        quant_e(0)
-        run(q0)
-        run(turn_in_unit(2))
-        sort_f(1)
+        consts_down()
+        run(qx)
         sort_fs(1)
-        for t in range(4):
-            stage1_wide(0, 4, 0, t)
+        banks = [bank() for t in range(4)]
+        first_passes(banks, 0, range(2))
+        qz = [turn_in(0, 2, 2), turn_in(2, 4, 2)]
+        sort_e(0)
         sort_e(1)
-        q2 = turn_in_unit(4)
+        first_passes(banks, 0, range(2, 4))
+        first_passes(banks, 1, range(4))
+        run(qz)
+        quant_e(0)
+        sort_f(1)
+        expo[0, 0] = staged("expo", [P, 4, 512], F32, 3)
+        for t in range(4):
+            first_passes(banks, 2, (t,))
+            nc.scalar.activation(out=expo[0, 0][:, t, :], in_=banks[t][:], func=ACT.Exp)
         quant_e(1)
+        q2 = turn_in_unit(4)
         qv = rates(c0, 0, 0, 2)
         stage1_wide(0, 4, 1, 0)
         stage1_wide(0, 4, 1, 1)
@@ -383,6 +413,8 @@ def tile_power_law_net_production_k6_kernel(
                 load_flow(k + 3)
             run(pending)
             late = []
+            if k == 0:
+                consts_across()
             for a, g in in_at.get(k, []):
                 late.append(turn_in(a, a + 2, g))
             for a, b in out_at.get(k, []):
@@ -410,35 +442,39 @@ def tile_power_law_net_production_k6_kernel(
         round_y(10)
         load_flow(15)
         run([qy[0], qv, qy[1]])
+        store_codes(8, 10)
+        store_scales(0, 10)
         stage2(11)
+        stage2(12, (0,))
         to_mass(11)
         round_y(11)
-        stage2(12)
+        stage2(12, (1,))
         qv = rates(last, 1, 14, 16)
         to_mass(12)
         qv()
         stage2(13)
         qy = [turn_out(10, 12, g) for g in range(2)]
         round_y(12)
+        stage2(14, (0,))
         to_mass(13)
         round_y(13)
-        stage2(14)
+        stage2(14, (1,))
+        stage2(15, (0,))
         to_mass(14)
-        run(qy)
-        store_codes(8, 12)
-        store_scales(0, 12)
-        stage2(15)
-        qy = [turn_out(12, 14, g) for g in range(2)]
         round_y(14)
+        stage2(15, (1,))
+        run(qy[:1])
         to_mass(15)
-        run(qy)
-        qy = [turn_out(14, 15, g) for g in range(2)]
+        run(qy[1:])
+        store_codes(10, 12)
+        qy = [turn_out(12, 14, 0), turn_out(12, 14, 1)]
         y_bf[15] = staged("y_bf", [P, S], BF16, 4)
-        round_half(15, 1, nc.scalar.copy)
         round_half(15, 0, nc.vector.tensor_copy)
+        qy2 = [turn_out(14, 15, 0, True), turn_out(14, 15, 1, True)]
+        round_half(15, 1, nc.scalar.copy)
         run(qy)
-        store_codes(12, 15)
-        qy = [turn_out(15, 16, 1), turn_out(15, 16, 0, True)]
-        run(qy)
-        store_codes(15, 16)
-        store_scales(12, 16)
+        store_codes(12, 14)
+        qy3 = [turn_out(15, 16, 0, True), turn_out(15, 16, 1)]
+        run(qy2 + qy3)
+        store_codes(14, 16, nc.scalar)
+        store_scales(10, 16)

@@ -17,32 +17,15 @@ ALU = mybir.AluOpType
 ACT = mybir.ActivationFunctionType
 
 P = 128
-TILES = B // P
-CHUNKS = [(0, 4), (4, 8), (8, 12), (12, 16)]
-IN_UNITS = [(0, 2), (2, 4), (4, 6), (6, 8), (8, 10), (10, 12), (12, 14), (14, 16)]
-OUT_UNITS = [(0, 2), (2, 4), (4, 6), (6, 8), (8, 10), (10, 12), (12, 14), (14, 15), (15, 16)]
-IN_LEAD = 5
-GCOLS = 704
-RATE_PSUM = False
-MM_BUFS = 4
-E_ON_V = (0,)
-YCOPY_V = ()
-CLAG = 5
-DLAG = 2
-XB = 8
-LASTG = 2
-SC_FIRST = True
-UNIT_PSUM = True
-TAILJ = 11
-GTAIL = 512
-IN_AT = {4: 1, 5: 2, 6: 4, 7: 6}
-S2FIRST = 13
-SPLIT = False
-GRP = 8
-IN_TICK = [-2, -1, 0, 1, 2, 3, 5, 7]
-S1_PER = [2, 2, 2, 2]
-RATE0 = 2
-YB = 5
+GROUP = 512
+CHUNK = 4
+
+STAGE1_LEAD = 5
+RATE_LEAD = 3
+LAST_STEP = 10
+TURN_IN_STEP = {1: 8, 2: 10, 4: 12, 6: 14}
+SORTED_PAIRS = (8, 10)
+POOL_COLS = 640
 
 
 def tile_power_law_net_production_k6_kernel(
@@ -61,222 +44,263 @@ def tile_power_law_net_production_k6_kernel(
         def staged(tag, shape, dtype, bufs):
             return work.tile(shape, dtype, name=tag, tag=tag, bufs=bufs, align_bytes=64)
 
-        def bank(tag="mm"):
-            return psum.tile([P, 512], F32, name=tag, tag=tag, bufs=MM_BUFS if tag == "mm" else 7 - MM_BUFS)
+        def sum_bank():
+            return psum.tile([P, GROUP], F32, name="sums", tag="sums", bufs=4)
+
+        def turn_bank():
+            return psum.tile([P, GROUP], F32, name="turns", tag="turns", bufs=3)
+
+        def wide_tile(shape, dtype):
+            return staged("wide", shape, dtype, 5)
+
+        def slot_tile():
+            return staged("slots", [P, 1024], BF16, 8)
+
+        def run(calls):
+            for call in calls:
+                call()
 
         ident = kept("ident", [P, P], F32)
         make_identity(nc, ident[:])
-        rows = kept("rows", [P, 512], BF16)
-        nc.vector.memset(rows[:], 0.0)
-        fs_raw = kept("fs_raw", [P, 2, R], U8)
-        p_sc = kept("p_sc", [P, 2, S], U8)
-        nc.vector.memset(fs_raw[:].rearrange("p g n -> p (g n)").bitcast(I32), 0)
-        nc.vector.memset(p_sc[:].rearrange("p g n -> p (g n)").bitcast(I32), 0)
-        warm = kept("warm", [P, 16], F32)
-        nc.vector.memset(warm[:, 0:8], 0.0)
-        nc.scalar.activation(out=warm[:, 8:16], in_=warm[:, 0:8], func=ACT.Exp)
+        const_rows = kept("const_rows", [P, GROUP], BF16)
+        nc.vector.memset(const_rows[:], 0.0)
+        f_plane_raw = kept("f_plane_raw", [P, 2, R], U8)
+        p_plane = kept("p_plane", [P, 2, S], U8)
+        nc.vector.memset(f_plane_raw[:].rearrange("p g c -> p (g c)").bitcast(I32), 0)
+        nc.vector.memset(p_plane[:].rearrange("p h c -> p (h c)").bitcast(I32), 0)
+        ident_bf = kept("ident_bf", [P, P], BF16)
+        nc.vector.tensor_copy(out=ident_bf[:], in_=ident[:])
 
         x_codes = [kept("x_codes%d" % g, [P, B], U32) for g in range(3)]
-        x_sc = [kept("x_sc%d" % g, [P, B], U8) for g in range(3)]
+        x_plane = [kept("x_plane%d" % g, [P, B], U8) for g in range(3)]
         v_codes = [kept("v_codes%d" % h, [P, B], U32) for h in range(2)]
-        v_sc = [kept("v_sc%d" % h, [P, B], U8) for h in range(2)]
+        v_plane = [kept("v_plane%d" % h, [P, B], U8) for h in range(2)]
         y_codes = kept("y_codes", [P, 2, B], U32)
-        y_sc = kept("y_sc", [P, 2, B], U8)
+        y_plane = kept("y_plane", [P, 2, B], U8)
 
-        x_raw, z_raw, flow, y_f32, y_bf, expo = {}, {}, {}, {}, {}, {}
+        logs, z_pair, sorted_words, flow, expo, y_f32, y_bf = {}, {}, {}, {}, {}, {}, {}
+        f_raw, f_codes, f_plane, e_raw, e_slots, e_codes, e_plane = {}, {}, {}, {}, {}, {}, {}
 
-        k_rows = {}
+        def load_first_chunk(g):
+            source = log_x[:GROUP, GROUP * g : GROUP * (g + 1)] if g < 2 else log_z[:GROUP, :]
+            four = kept("first%d" % g, [P, CHUNK, GROUP], BF16)
+            nc.sync.dma_start(out=four[:], in_=source.rearrange("(j p) k -> p j k", j=CHUNK))
+            for j in range(CHUNK):
+                logs[j, g] = four[:, j, :]
 
-        def load_first(g):
-            src = log_x[:512, 512 * g : 512 * (g + 1)] if g < 2 else log_z[:512, :]
-            four = kept("first%d" % g, [P, 4, 512], BF16)
-            nc.sync.dma_start(out=four[:], in_=src.rearrange("(i p) k -> p i k", i=4))
-            for j in range(4):
-                k_rows[j, g] = four[:, j, :]
-
-        def load_x(j):
-            x_raw[j] = staged("x_raw", [P, S], BF16, XB)
-            nc.sync.dma_start(out=x_raw[j][:], in_=log_x[j * P : (j + 1) * P, :])
-            k_rows[j, 0], k_rows[j, 1] = x_raw[j][:, :512], x_raw[j][:, 512:]
-
-        def load_z(j):
-            pair = staged("z_raw", [P, 2, Z], BF16, XB // 2)
-            nc.sync.dma_start(out=pair[:], in_=log_z[j * P : (j + 2) * P, :].rearrange("(i p) k -> p i k", i=2))
-            k_rows[j, 2], k_rows[j + 1, 2] = pair[:, 0, :], pair[:, 1, :]
-
-        def load_in(j):
-            load_x(j)
-            load_x(j + 1)
-            load_z(j)
+        def load_pair(a):
+            for j in (a, a + 1):
+                x_tile = staged("x_tile", [P, S], BF16, 8)
+                nc.sync.dma_start(out=x_tile[:], in_=log_x[j * P : (j + 1) * P, :])
+                logs[j, 0], logs[j, 1] = x_tile[:, :GROUP], x_tile[:, GROUP:]
+            z_pair[a] = staged("z_pair", [P, 2, Z], BF16, 4)
+            nc.sync.dma_start(out=z_pair[a][:], in_=log_z[a * P : (a + 2) * P, :].rearrange("(j p) k -> p j k", j=2))
+            logs[a, 2], logs[a + 1, 2] = z_pair[a][:, 0, :], z_pair[a][:, 1, :]
 
         def load_flow(j):
             flow[j] = staged("flow", [P, S], BF16, 5)
             nc.sync.dma_start(out=flow[j][:], in_=inflow[j * P : (j + 1) * P, :])
 
-        def load_scales(plane, rows):
+        def load_planes(plane, scale_rows):
             for q in range(4):
                 nc.sync.dma_start(
                     out=plane[32 * q : 32 * q + 4, :, :].bitcast(I32),
-                    in_=rows[:, 4 * q : 4 * q + 4, :].rearrange("g r n -> r g n").bitcast(I32),
+                    in_=scale_rows[:, 4 * q : 4 * q + 4, :].rearrange("g r c -> r g c").bitcast(I32),
                 )
 
-        f_raw, e_raw, f_codes, f_sc, e_grp, e_codes, e_sc = {}, {}, {}, {}, {}, {}, {}
-
         def load_f(h):
-            f_raw[h] = kept("f_raw%d" % h, [P, 2, 1024], U8)
+            f_raw[h] = kept("f_raw%d" % h, [P, 2, 2 * GROUP], U8)
             nc.sync.dma_start(
                 out=f_raw[h][:].bitcast(I32),
-                in_=f_words[:, :, 1024 * h : 1024 * (h + 1)].rearrange("g p b -> p g b").bitcast(I32),
+                in_=f_words[:, :, 2 * GROUP * h : 2 * GROUP * (h + 1)].rearrange("g p b -> p g b").bitcast(I32),
             )
 
         def load_e(h):
-            e_raw[h] = staged("y_f32", [P, 4, 512], BF16, YB)
+            e_raw[h] = wide_tile([P, 4, GROUP], BF16)
             nc.sync.dma_start(
-                out=e_raw[h][:], in_=e_orders[:, 512 * h : 512 * (h + 1)].rearrange("(p j) c -> p j c", j=4)
+                out=e_raw[h][:], in_=e_orders[:, GROUP * h : GROUP * (h + 1)].rearrange("(p s) c -> p s c", s=4)
             )
 
-        def sort_f(h):
-            f_codes[h] = kept("f_codes%d" % h, [P, 2, 1024], U8)
+        def sort_f_codes(h):
+            f_codes[h] = kept("f_codes%d" % h, [P, 2, 2 * GROUP], U8)
             nc.vector.tensor_copy(
                 out=f_codes[h][:].rearrange("p g (t m b) -> p g t m b", t=4, b=2),
                 in_=f_raw[h][:].rearrange("p g (m t b) -> p g t m b", t=4, b=2),
             )
 
-        def sort_fs(h):
-            f_sc[h] = kept("f_sc%d" % h, [P, 2, 512], U8)
+        def sort_f_plane(h):
+            f_plane[h] = kept("f_plane%d" % h, [P, 2, GROUP], U8)
             nc.vector.tensor_copy(
-                out=f_sc[h][:].rearrange("p g (t m) -> p g t m", t=4),
-                in_=fs_raw[:, :, 512 * h : 512 * (h + 1)].rearrange("p g (m t) -> p g t m", t=4),
+                out=f_plane[h][:].rearrange("p g (t m) -> p g t m", t=4),
+                in_=f_plane_raw[:, :, GROUP * h : GROUP * (h + 1)].rearrange("p g (m t) -> p g t m", t=4),
             )
 
         def sort_e(h):
-            e_grp[h] = staged("y_f32", [P, 2048], BF16, YB)
-            dst = e_grp[h][:].rearrange("p (t a b j) -> p a t b j", t=4, b=2, j=4)
-            src = e_raw[h][:].rearrange("p j (a b t) -> p a t b j", b=2, t=4)
-            if h in E_ON_V:
-                nc.vector.tensor_copy(out=dst, in_=src)
-            else:
-                nc.scalar.copy(out=dst, in_=src)
-
-        def quant_e(h):
-            e_codes[h] = kept("e_codes%d" % h, [P, 512], U32)
-            e_sc[h] = kept("e_sc%d" % h, [P, 512], U8)
-            nc.vector.quantize_mx(out=e_codes[h][:].bitcast(FP8X4), scales=e_sc[h][:], in_=e_grp[h][:])
-
-        def turn(words_of, tiles, step, on_vector):
-            n = len(tiles)
-            ps = bank("tp")
-            for i, j in enumerate(tiles):
-                for u in range(2):
-                    nc.tensor.transpose(ps[:, (2 * i + u) * P : (2 * i + u + 1) * P], words_of(j, u), ident[:])
-            grp = staged("grp", [P, 1024], BF16, GRP)
-            dst = grp[:, : n * 512].bitcast(F32).rearrange("p (i c u) -> p i c u", i=n, u=2)
-            src = ps[:, : n * 256].rearrange("p (i u c) -> p i c u", i=n, u=2)
-            if on_vector:
-                nc.vector.tensor_copy(out=dst, in_=src)
-            else:
-                nc.scalar.copy(out=dst, in_=src)
-            return grp
-
-        def quant(grp, codes, scales, a, b):
-            nc.vector.quantize_mx(
-                out=codes[:, a * P : b * P].bitcast(FP8X4), scales=scales[:, a * P : b * P], in_=grp[:, : (b - a) * 512]
+            e_slots[h] = wide_tile([P, 4 * GROUP], BF16)
+            nc.vector.tensor_copy(
+                out=e_slots[h][:].rearrange("p (t a b s) -> p a t b s", t=4, b=2, s=4),
+                in_=e_raw[h][:].rearrange("p s (a b t) -> p a t b s", b=2, t=4),
             )
 
-        def turn_in(a, b, g):
-            grp = turn(lambda j, u: k_rows[j, g].bitcast(F32)[:, u:256:2], range(a, b), 2, False)
-            return lambda: quant(grp, x_codes[g], x_sc[g], a, b)
+        def quantise_e(h):
+            e_codes[h] = kept("e_codes%d" % h, [P, GROUP], U32)
+            e_plane[h] = kept("e_plane%d" % h, [P, GROUP], U8)
+            nc.vector.quantize_mx(out=e_codes[h][:].bitcast(FP8X4), scales=e_plane[h][:], in_=e_slots[h][:])
 
-        def turn_out(a, b, g, on_v=False):
-            grp = turn(
-                lambda j, u: y_bf[j][:].bitcast(F32)[:, (2 * g + u) * P : (2 * g + u + 1) * P], range(a, b), 1, on_v
-            )
-            return lambda: quant(grp, y_codes[:, g, :], y_sc[:, g, :], a, b)
+        consts = psum.tile([P, 2 * GROUP], BF16, name="consts", tag="consts")
+        unit_high = consts[:, GROUP:]
+        unit_down = kept("unit_down", [P, 4, 2], BF16)
+        unit_low = kept("unit_low", [P, POOL_COLS], BF16)
 
-        def log_rate_passes(out, h, t, a, b, gs=(0, 1, 2)):
-            cells = slice(a * P, b * P)
-            for g in gs:
-                if g < 2:
-                    w = f_codes[h][:, g, 256 * t : 256 * (t + 1)].bitcast(FP4X4)
-                    ws = f_sc[h][:, g, P * t : P * (t + 1)]
-                else:
-                    w = e_codes[h][:, P * t : P * (t + 1)].bitcast(FP8X4)
-                    ws = e_sc[h][:, P * t : P * (t + 1)]
-                nc.tensor.matmul_mx(
-                    out=out, lhsT=w, lhsT_scale=ws, rhs=x_codes[g][:, cells].bitcast(FP8X4), rhs_scale=x_sc[g][:, cells],
-                    start=(g == 0), stop=(g == LASTG),
-                )
-
-        def stage1_wide(a, b, h, t):
-            if t == 0:
-                expo[a, h] = staged("expo", [P, 4, 512], F32, 3)
-            ps = bank()
-            log_rate_passes(ps[:], h, t, a, b)
-            nc.scalar.activation(out=expo[a, h][:, t, :], in_=ps[:], func=ACT.Exp)
-
-        def stage1_narrow(a, h):
-            expo[a, h] = staged("expo_n", [P, 1, 512], F32, 4)
-            ps = bank()
+        def turn_constants_down():
             for t in range(4):
-                log_rate_passes(ps[:, t * P : (t + 1) * P], h, t, a, a + 1)
-            nc.scalar.activation(
-                out=expo[a, h][:, 0, :].rearrange("p (c t) -> p c t", t=4),
-                in_=ps[:].rearrange("p (t c) -> p c t", t=4), func=ACT.Exp,
+                nc.tensor.transpose(consts[:, t * P : (t + 1) * P], const_rows[:, t:GROUP:4], ident_bf[:])
+            bank = turn_bank()[:].bitcast(BF16)
+            for c in range(4):
+                nc.tensor.transpose(bank[:, c * P : (c + 1) * P], const_rows[:, c * P : (c + 1) * P], ident_bf[:])
+            nc.scalar.copy(out=unit_down[:], in_=bank[:, :GROUP].rearrange("p (c r) -> p c r", c=4)[:, :, 2:4])
+
+        def spread_unit():
+            bank = turn_bank()[:].bitcast(BF16)
+            for c in range(POOL_COLS // P):
+                column = unit_down[:, c % 4, c // 4 : c // 4 + 1]
+                nc.tensor.transpose(bank[:, c * P : (c + 1) * P], column.to_broadcast([P, P]), ident_bf[:])
+            for c in range(4):
+                column = unit_down[:, c, 1:2]
+                nc.tensor.transpose(unit_high[:, c * P : (c + 1) * P], column.to_broadcast([P, P]), ident_bf[:])
+            nc.scalar.copy(out=unit_low[:], in_=bank[:, :POOL_COLS])
+
+        def quantise(slots, codes, plane, a, b):
+            nc.vector.quantize_mx(
+                out=codes[:, a * P : b * P].bitcast(FP8X4), scales=plane[:, a * P : b * P], in_=slots[:, : (b - a) * GROUP]
             )
 
-        def rates(chunk, h, a, b):
-            grp = staged("grp", [P, 1024], BF16, GRP)
-            n = (b - a) * P
-            if chunk[1] - chunk[0] == 1:
-                nc.vector.tensor_tensor(
-                    out=grp[:, :512].rearrange("p (c t) -> p c t", t=4),
-                    in0=expo[a, h][:, 0, :].rearrange("p (c t) -> p c t", t=4),
-                    in1=rate_of(h).unsqueeze(1).to_broadcast([P, P, 4]), op=ALU.mult,
-                )
-            else:
-                c0 = (a - chunk[0]) * P
-                nc.vector.tensor_tensor(
-                    out=grp[:, : 4 * n].rearrange("p (c i t) -> p c t i", i=2, t=4),
-                    in0=expo[chunk[0], h][:, :, c0 : c0 + n].rearrange("p t (c i) -> p c t i", i=2),
-                    in1=rate_of(h).unsqueeze(1).unsqueeze(3).to_broadcast([P, n // 2, 4, 2]), op=ALU.mult,
-                )
-            return lambda: quant(grp, v_codes[h], v_sc[h], a, b)
+        def turn(words_of, a, b, copy):
+            count = b - a
+            bank = turn_bank()
+            for j in range(a, b):
+                for u in range(2):
+                    place = 2 * (j - a) + u
+                    nc.tensor.transpose(bank[:, place * P : (place + 1) * P], words_of(j, u), ident[:])
+            slots = slot_tile()
+            copy(
+                out=slots[:, : count * GROUP].bitcast(F32).rearrange("p (j c u) -> p j c u", j=count, u=2),
+                in_=bank[:, : count * 2 * P].rearrange("p (j u c) -> p j c u", j=count, u=2),
+            )
+            return slots
 
-        def gcols(j):
-            return GCOLS if j < TAILJ else GTAIL
-
-        def stage2(j, halves=(0, 1)):
-            if 0 in halves:
-                y_f32[j] = staged("y_f32", [P, S], F32, YB)
-            cells = slice(j * P, (j + 1) * P)
-            for n in halves:
-                cols = slice(512 * n, 512 * (n + 1))
-                ps = bank()
-                for h in range(2):
-                    nc.tensor.matmul_mx(
-                        out=ps[:], lhsT=v_codes[h][:, cells].bitcast(FP8X4), lhsT_scale=v_sc[h][:, cells],
-                        rhs=p_codes[:, h, cols].bitcast(FP8X4), rhs_scale=p_sc[:, h, cols], start=(h == 0), stop=(h == 1),
+        def sort_words(a):
+            for g in range(3):
+                words = staged("words", [P, 2, 2 * P], F32, 6)
+                if g < 2:
+                    for j in range(2):
+                        nc.vector.tensor_copy(
+                            out=words[:, j, :].rearrange("p (u c r) -> p c u r", u=2, r=4),
+                            in_=logs[a + j, g].bitcast(F32).rearrange("p (c r u) -> p c u r", u=2, r=4),
+                        )
+                else:
+                    nc.vector.tensor_copy(
+                        out=words[:].rearrange("p j (u c r) -> p j c u r", u=2, r=4),
+                        in_=z_pair[a][:].bitcast(F32).rearrange("p j (c r u) -> p j c u r", u=2, r=4),
                     )
-                nc.vector.tensor_tensor(out=y_f32[j][:, cols], in0=ps[:], in1=flow[j][:, cols], op=ALU.add)
-                lo, hi = 512 * n, min(512 * (n + 1), gcols(j))
-                if hi > lo:
-                    nc.gpsimd.tensor_tensor(out=y_f32[j][:, lo:hi], in0=y_f32[j][:, lo:hi], in1=unit_bc[:, lo:hi], op=ALU.mult)
+                sorted_words[a, g] = words
+
+        def turn_in(a, g):
+            if a in SORTED_PAIRS:
+                slots = turn(lambda j, u: sorted_words[a, g][:, j - a, u * P : (u + 1) * P], a, a + 2, nc.scalar.copy)
+            else:
+                slots = turn(lambda j, u: logs[j, g].bitcast(F32)[:, u : 2 * P : 2], a, a + 2, nc.scalar.copy)
+            return lambda: quantise(slots, x_codes[g], x_plane[g], a, a + 2)
+
+        def turn_in_pair(a):
+            return [turn_in(a, g) for g in range(3)]
+
+        def turn_out(a, b, n, copy=nc.scalar.copy):
+            slots = turn(lambda j, u: y_bf[j][:].bitcast(F32)[:, (2 * n + u) * P : (2 * n + u + 1) * P], a, b, copy)
+            return lambda: quantise(slots, y_codes[:, n, :], y_plane[:, n, :], a, b)
+
+        def turn_out_pair(a):
+            return [turn_out(a, a + 2, n) for n in range(2)]
+
+        def exponent_pass(bank, a, h, t, g):
+            cells = slice(a * P, (a + CHUNK) * P)
+            if g < 2:
+                orders = f_codes[h][:, g, 2 * P * t : 2 * P * (t + 1)].bitcast(FP4X4)
+                orders_plane = f_plane[h][:, g, P * t : P * (t + 1)]
+            else:
+                orders = e_codes[h][:, P * t : P * (t + 1)].bitcast(FP8X4)
+                orders_plane = e_plane[h][:, P * t : P * (t + 1)]
+            nc.tensor.matmul_mx(
+                out=bank[:], lhsT=orders, lhsT_scale=orders_plane,
+                rhs=x_codes[g][:, cells].bitcast(FP8X4), rhs_scale=x_plane[g][:, cells],
+                start=(g == 0), stop=(g == 2),
+            )
+
+        def exponential(bank, a, h, t):
+            if t == 0:
+                expo[a, h] = staged("expo", [P, 4, GROUP], F32, 3)
+            nc.scalar.activation(out=expo[a, h][:, t, :], in_=bank[:], func=ACT.Exp)
+
+        def stage1(a, h, t):
+            bank = sum_bank()
+            for g in range(3):
+                exponent_pass(bank, a, h, t, g)
+            exponential(bank, a, h, t)
+
+        def rates(a, h):
+            first = a - a % CHUNK
+            cells = slice((a - first) * P, (a - first + 2) * P)
+            rate = consts[:, :GROUP].rearrange("p (t r) -> p t r", t=4)[:, :, h]
+            slots = slot_tile()
+            nc.vector.tensor_tensor(
+                out=slots[:].rearrange("p (c i t) -> p c t i", i=2, t=4),
+                in0=expo[first, h][:, :, cells].rearrange("p t (c i) -> p c t i", i=2),
+                in1=rate.unsqueeze(1).unsqueeze(3).to_broadcast([P, P, 4, 2]),
+                op=ALU.mult,
+            )
+            return lambda: quantise(slots, v_codes[h], v_plane[h], a, a + 2)
+
+        def pool_cols(j):
+            return POOL_COLS if j <= LAST_STEP else GROUP
+
+        def stage2_half(j, n):
+            if n == 0:
+                y_f32[j] = wide_tile([P, S], F32)
+            cells = slice(j * P, (j + 1) * P)
+            cols = slice(GROUP * n, GROUP * (n + 1))
+            bank = sum_bank()
+            for h in range(2):
+                nc.tensor.matmul_mx(
+                    out=bank[:], lhsT=v_codes[h][:, cells].bitcast(FP8X4), lhsT_scale=v_plane[h][:, cells],
+                    rhs=p_codes[:, h, cols].bitcast(FP8X4), rhs_scale=p_plane[:, h, cols],
+                    start=(h == 0), stop=(h == 1),
+                )
+            nc.vector.tensor_tensor(out=y_f32[j][:, cols], in0=bank[:], in1=flow[j][:, cols], op=ALU.add)
+            share = slice(GROUP * n, min(GROUP * (n + 1), pool_cols(j)))
+            if share.stop > share.start:
+                nc.gpsimd.tensor_tensor(out=y_f32[j][:, share], in0=y_f32[j][:, share], in1=unit_low[:, share], op=ALU.mult)
+
+        def stage2(j):
+            stage2_half(j, 0)
+            stage2_half(j, 1)
 
         def to_mass(j):
-            c = gcols(j)
-            if c < S:
-                nc.vector.tensor_tensor(out=y_f32[j][:, c:], in0=y_f32[j][:, c:], in1=unit_hi[:, c - 512 :], op=ALU.mult)
+            c = pool_cols(j)
+            nc.vector.tensor_tensor(out=y_f32[j][:, c:], in0=y_f32[j][:, c:], in1=unit_high[:, c - GROUP :], op=ALU.mult)
 
-        def round_y(j):
-            nc.sync.dma_start(out=out_0[j * P : (j + 1) * P, :], in_=y_f32[j][:])
+        def new_y_bf(j):
             y_bf[j] = staged("y_bf", [P, S], BF16, 4)
+
+        def store_and_round(j):
+            nc.sync.dma_start(out=out_0[j * P : (j + 1) * P, :], in_=y_f32[j][:])
+            new_y_bf(j)
             nc.scalar.copy(
-                out=y_bf[j][:].rearrange("p (g u q e) -> p g u q e", g=2, u=2, e=2),
-                in_=y_f32[j][:].rearrange("p (g q u e) -> p g u q e", g=2, u=2, e=2),
+                out=y_bf[j][:].rearrange("p (n u q e) -> p n u q e", n=2, u=2, e=2),
+                in_=y_f32[j][:].rearrange("p (n q u e) -> p n u q e", n=2, u=2, e=2),
             )
 
-        def round_half(j, g, copy):
-            cols = slice(512 * g, 512 * (g + 1))
+        def store_and_round_half(j, n, copy):
+            cols = slice(GROUP * n, GROUP * (n + 1))
             nc.sync.dma_start(out=out_0[j * P : (j + 1) * P, cols], in_=y_f32[j][:, cols])
             copy(
                 out=y_bf[j][:, cols].rearrange("p (u q e) -> p u q e", u=2, e=2),
@@ -285,196 +309,139 @@ def tile_power_law_net_production_k6_kernel(
 
         def store_codes(a, b, queue=nc.sync):
             queue.dma_start(
-                out=out_1[:, :, a * P : b * P, :].rearrange("g p m t -> p g (m t)").bitcast(I32),
+                out=out_1[:, :, a * P : b * P, :].rearrange("n p c t -> p n (c t)").bitcast(I32),
                 in_=y_codes[:, :, a * P : b * P].bitcast(I32),
             )
 
-        def store_scales(a, b):
+        def store_planes(a, b):
             for q in range(4):
                 nc.sync.dma_start(
-                    out=out_2[:, 4 * q : 4 * q + 4, a * P : b * P].rearrange("g r m -> r g m").bitcast(I32),
-                    in_=y_sc[32 * q : 32 * q + 4, :, a * P : b * P].bitcast(I32),
+                    out=out_2[:, 4 * q : 4 * q + 4, a * P : b * P].rearrange("n r c -> r n c").bitcast(I32),
+                    in_=y_plane[32 * q : 32 * q + 4, :, a * P : b * P].bitcast(I32),
                 )
 
-        ident_bf = kept("ident_bf", [P, P], BF16)
-        nc.vector.tensor_copy(out=ident_bf[:], in_=ident[:])
-        load_first(0)
+        load_first_chunk(0)
         load_f(0)
-        load_first(1)
-        load_scales(fs_raw, f_scales)
-        nc.sync.dma_start(out=rows[0:2, :], in_=rate_const.rearrange("(h n) -> h n", h=2))
-        nc.sync.dma_start(out=rows[2:4, :], in_=unit.rearrange("(h n) -> h n", h=2))
-        load_first(2)
+        load_first_chunk(1)
+        load_planes(f_plane_raw, f_scales)
+        nc.sync.dma_start(out=const_rows[0:2, :], in_=rate_const.rearrange("(h c) -> h c", h=2))
+        nc.sync.dma_start(out=const_rows[2:4, :], in_=unit.rearrange("(n c) -> n c", n=2))
+        load_first_chunk(2)
         load_e(0)
         load_f(1)
         load_e(1)
-        load_in(4)
-        load_in(6)
+        load_pair(4)
+        load_pair(6)
         p_codes = kept("p_codes", [P, 2, S], U32)
-        nc.sync.dma_start(out=p_codes[:].bitcast(I32), in_=p_words.rearrange("g p n t -> p g (n t)").bitcast(I32))
-        load_scales(p_sc, p_scales)
+        nc.sync.dma_start(out=p_codes[:].bitcast(I32), in_=p_words.rearrange("h p c t -> p h (c t)").bitcast(I32))
+        load_planes(p_plane, p_scales)
         load_flow(0)
         load_flow(1)
 
-        def turn_in_unit(a):
-            return [turn_in(a, a + 2, g) for g in range(3)]
-
-        def run(todos):
-            for todo in todos:
-                todo()
-
-        consts = psum.tile([P, 1024], BF16, name="consts", tag="consts")
-        rate_of = lambda h: consts[:, :512].rearrange("p (t r) -> p t r", t=4)[:, :, h]
-        unit_hi = consts[:, 512:]
-        unit_col = kept("unit_col", [P, 4, 2], BF16)
-        unit_bc = kept("unit_bc", [P, S], BF16)
-
-        def consts_down():
-            for t in range(4):
-                nc.tensor.transpose(consts[:, t * P : (t + 1) * P], rows[:, t:512:4], ident_bf[:])
-            ps = bank("tp")
-            cols_ps = ps[:].bitcast(BF16)
-            for c in range(4):
-                nc.tensor.transpose(cols_ps[:, c * P : (c + 1) * P], rows[:, c * P : (c + 1) * P], ident_bf[:])
-            nc.scalar.copy(out=unit_col[:], in_=cols_ps[:, :512].rearrange("p (c r) -> p c r", c=4)[:, :, 2:4])
-
-        def consts_across():
-            ps = bank("tp")
-            unit_ps = ps[:].bitcast(BF16)
-            for c in range(8):
-                nc.tensor.transpose(
-                    unit_ps[:, c * P : (c + 1) * P], unit_col[:, c % 4, c // 4 : c // 4 + 1].to_broadcast([P, P]), ident_bf[:]
-                )
-            for c in range(4):
-                nc.tensor.transpose(unit_hi[:, c * P : (c + 1) * P], unit_col[:, c, 1:2].to_broadcast([P, P]), ident_bf[:])
-            nc.scalar.copy(out=unit_bc[:], in_=unit_ps)
-
-        def first_passes(banks, g, ts):
-            for t in ts:
-                log_rate_passes(banks[t][:], 0, t, 0, 4, (g,))
-
-        c0 = CHUNKS[0]
-        qx = [turn_in(0, 2, 0), turn_in(2, 4, 0)]
-        sort_f(0)
-        run(qx)
-        qx = [turn_in(0, 2, 1), turn_in(2, 4, 1)]
-        sort_fs(0)
-        consts_down()
-        run(qx)
-        sort_fs(1)
-        banks = [bank() for t in range(4)]
-        first_passes(banks, 0, range(2))
-        qz = [turn_in(0, 2, 2), turn_in(2, 4, 2)]
+        quantise_x = [turn_in(0, 0), turn_in(2, 0)]
+        sort_f_codes(0)
+        run(quantise_x)
+        quantise_x = [turn_in(0, 1), turn_in(2, 1)]
+        sort_f_plane(0)
+        turn_constants_down()
+        run(quantise_x)
+        sort_f_plane(1)
+        banks = [sum_bank() for t in range(4)]
+        for t in (0, 1):
+            exponent_pass(banks[t], 0, 0, t, 0)
+        quantise_x = [turn_in(0, 2), turn_in(2, 2)]
         sort_e(0)
-        sort_e(1)
-        first_passes(banks, 0, range(2, 4))
-        first_passes(banks, 1, range(4))
-        run(qz)
-        quant_e(0)
-        sort_f(1)
-        expo[0, 0] = staged("expo", [P, 4, 512], F32, 3)
+        for t in (2, 3):
+            exponent_pass(banks[t], 0, 0, t, 0)
         for t in range(4):
-            first_passes(banks, 2, (t,))
-            nc.scalar.activation(out=expo[0, 0][:, t, :], in_=banks[t][:], func=ACT.Exp)
-        quant_e(1)
-        q2 = turn_in_unit(4)
-        qv = rates(c0, 0, 0, 2)
-        stage1_wide(0, 4, 1, 0)
-        stage1_wide(0, 4, 1, 1)
-        run(q2)
-        qv()
-        qv = rates(c0, 0, 2, 4)
-        q3 = turn_in_unit(6)
-        stage1_wide(0, 4, 1, 2)
-        stage1_wide(0, 4, 1, 3)
-        run(q3)
-        qv()
+            exponent_pass(banks[t], 0, 0, t, 1)
+        quantise_e(0)
+        run(quantise_x)
+        sort_f_codes(1)
+        sort_e(1)
+        for t in range(4):
+            exponent_pass(banks[t], 0, 0, t, 2)
+            exponential(banks[t], 0, 0, t)
+        quantise_e(1)
 
-        in_at, s1_at, rate_at, out_at = {}, {}, {}, {}
-        for u, k in IN_AT.items():
-            in_at.setdefault(k, []).extend([(2 * u, 0), (2 * u, 1), (2 * u, 2)])
-        for a, b in CHUNKS:
-            for i in range(8):
-                if a > 0:
-                    s1_at.setdefault(a - 5 + i // 2, []).append((a, b, i // 4, i % 4))
-            for i in range(4):
-                lo = a + 2 * (i % 2)
-                if a > 0 or i > 1:
-                    rate_at.setdefault(a - 3 + i, []).append(((a, b), i // 2, lo, lo + 2))
-        for a, b in OUT_UNITS:
-            out_at.setdefault(b - 1 + DLAG, []).append((a, b))
+        quantise_x = turn_in_pair(4)
+        quantise_v = rates(0, 0)
+        stage1(0, 1, 0)
+        stage1(0, 1, 1)
+        run(quantise_x + [quantise_v])
+        quantise_v = rates(2, 0)
+        quantise_x = turn_in_pair(6)
+        stage1(0, 1, 2)
+        stage1(0, 1, 3)
+        run(quantise_x + [quantise_v])
 
-        pending = []
-        for k in range(-1, 11):
-            for a, g in in_at.get(k + 2, []):
-                if g == 0 and a >= 8:
-                    load_in(a)
-            if 2 <= k + 3 < TILES:
-                load_flow(k + 3)
-            run(pending)
-            late = []
+        waiting = []
+        for k in range(-1, LAST_STEP + 1):
+            if k + 2 in TURN_IN_STEP:
+                load_pair(TURN_IN_STEP[k + 2])
+            load_flow(k + 3)
+            run(waiting)
+            waiting = []
+            if TURN_IN_STEP.get(k + 1) in SORTED_PAIRS:
+                sort_words(TURN_IN_STEP[k + 1])
             if k == 0:
-                consts_across()
-            for a, g in in_at.get(k, []):
-                late.append(turn_in(a, a + 2, g))
-            for a, b in out_at.get(k, []):
-                for g in range(2):
-                    late.append(turn_out(a, b, g))
-                if b % 4 == 0:
-                    late.append(lambda b=b: store_codes(b - 4, b))
-            if 0 <= k - 1:
-                round_y(k - 1)
-            if 0 <= k:
+                spread_unit()
+            if k in TURN_IN_STEP:
+                waiting.extend(turn_in_pair(TURN_IN_STEP[k]))
+            if k >= 3 and k % 2 == 1:
+                waiting.extend(turn_out_pair(k - 3))
+                if (k - 1) % CHUNK == 0:
+                    waiting.append(lambda end=k - 1: store_codes(end - CHUNK, end))
+            if k >= 1:
+                store_and_round(k - 1)
+            if k >= 0:
                 stage2(k)
-            for chunk, h, a, b in rate_at.get(k, []):
-                late.insert(1, rates(chunk, h, a, b))
-            if 0 <= k:
+            chunk, piece = divmod(k + RATE_LEAD, CHUNK)
+            waiting.insert(1, rates(CHUNK * chunk + 2 * (piece % 2), piece // 2))
+            if k >= 0:
                 to_mass(k)
-            for a, b, h, t in s1_at.get(k, []):
-                stage1_wide(a, b, h, t)
-            pending = late
+            chunk, piece = divmod(k + STAGE1_LEAD, CHUNK)
+            for t in (2 * (piece % 2), 2 * (piece % 2) + 1):
+                stage1(CHUNK * chunk, piece // 2, t)
 
-        last = CHUNKS[-1]
         load_flow(14)
-        run(pending)
-        qy = [turn_out(8, 10, g) for g in range(2)]
-        qv = rates(last, 1, 12, 14)
-        round_y(10)
+        run(waiting)
+        quantise_y = turn_out_pair(8)
+        quantise_v = rates(12, 1)
+        store_and_round(10)
         load_flow(15)
-        run([qy[0], qv, qy[1]])
+        run([quantise_y[0], quantise_v, quantise_y[1]])
         store_codes(8, 10)
-        store_scales(0, 10)
+        store_planes(0, 10)
         stage2(11)
-        stage2(12, (0,))
+        stage2_half(12, 0)
         to_mass(11)
-        round_y(11)
-        stage2(12, (1,))
-        qv = rates(last, 1, 14, 16)
+        store_and_round(11)
+        stage2_half(12, 1)
+        quantise_v = rates(14, 1)
         to_mass(12)
-        qv()
+        quantise_v()
         stage2(13)
-        qy = [turn_out(10, 12, g) for g in range(2)]
-        round_y(12)
-        stage2(14, (0,))
-        to_mass(13)
-        round_y(13)
-        stage2(14, (1,))
-        stage2(15, (0,))
-        to_mass(14)
-        round_y(14)
-        stage2(15, (1,))
-        run(qy[:1])
+        quantise_y = turn_out_pair(10)
+        store_and_round(12)
+        for j in (13, 14):
+            stage2_half(j + 1, 0)
+            to_mass(j)
+            store_and_round(j)
+            stage2_half(j + 1, 1)
+        quantise_y[0]()
         to_mass(15)
-        run(qy[1:])
+        quantise_y[1]()
         store_codes(10, 12)
-        qy = [turn_out(12, 14, 0), turn_out(12, 14, 1)]
-        y_bf[15] = staged("y_bf", [P, S], BF16, 4)
-        round_half(15, 0, nc.vector.tensor_copy)
-        qy2 = [turn_out(14, 15, 0, True), turn_out(14, 15, 1, True)]
-        round_half(15, 1, nc.scalar.copy)
-        run(qy)
+
+        quantise_y = turn_out_pair(12)
+        new_y_bf(15)
+        store_and_round_half(15, 0, nc.vector.tensor_copy)
+        quantise_14 = [turn_out(14, 15, n, nc.vector.tensor_copy) for n in range(2)]
+        store_and_round_half(15, 1, nc.scalar.copy)
+        run(quantise_y)
         store_codes(12, 14)
-        qy3 = [turn_out(15, 16, 0, True), turn_out(15, 16, 1)]
-        run(qy2 + qy3)
+        quantise_15 = [turn_out(15, 16, 0, nc.vector.tensor_copy), turn_out(15, 16, 1)]
+        run(quantise_14 + quantise_15)
         store_codes(14, 16, nc.scalar)
-        store_scales(10, 16)
+        store_planes(10, 16)

from contextlib import ExitStack

import concourse.mybir as mybir
from concourse.masks import make_identity

B, S, Z, R = 2048, 1024, 512, 1024
FLOPS = 2 * B * (S * R + Z * R + R * S)

F32 = mybir.dt.float32
BF16 = mybir.dt.bfloat16
U32 = mybir.dt.uint32
I32 = mybir.dt.int32
U8 = mybir.dt.uint8
FP8X4 = mybir.dt.float8_e4m3fn_x4
FP4X4 = mybir.dt.float4_e2m1fn_x4
ALU = mybir.AluOpType
ACT = mybir.ActivationFunctionType

P = 128
GROUP = 512
CHUNK = 4

STAGE1_LEAD = 5
RATE_LEAD = 3
LAST_STEP = 10
TURN_IN_STEP = {1: 8, 2: 10, 4: 12, 6: 14}
SORTED_PAIRS = (8, 10)
POOL_COLS = 640


def tile_power_law_net_production_k6_kernel(
    tc, log_x, log_z, f_words, f_scales, e_orders, rate_const, p_words, p_scales, inflow, unit, out_0, out_1, out_2
):
    nc = tc.nc
    with ExitStack() as ctx:
        keep = ctx.enter_context(tc.tile_pool(name="keep", bufs=1))
        work = ctx.enter_context(tc.tile_pool(name="work", bufs=2))
        psum = ctx.enter_context(tc.psum_pool(name="psum", bufs=1))
        ctx.enter_context(tc.manual_schedule())

        def kept(name, shape, dtype):
            return keep.tile(shape, dtype, name=name, align_bytes=64)

        def staged(tag, shape, dtype, bufs):
            return work.tile(shape, dtype, name=tag, tag=tag, bufs=bufs, align_bytes=64)

        def sum_bank():
            return psum.tile([P, GROUP], F32, name="sums", tag="sums", bufs=4)

        def turn_bank():
            return psum.tile([P, GROUP], F32, name="turns", tag="turns", bufs=3)

        def wide_tile(shape, dtype):
            return staged("wide", shape, dtype, 5)

        def slot_tile():
            return staged("slots", [P, 1024], BF16, 8)

        def run(calls):
            for call in calls:
                call()

        ident = kept("ident", [P, P], F32)
        make_identity(nc, ident[:])
        const_rows = kept("const_rows", [P, GROUP], BF16)
        nc.vector.memset(const_rows[:], 0.0)
        f_plane_raw = kept("f_plane_raw", [P, 2, R], U8)
        p_plane = kept("p_plane", [P, 2, S], U8)
        nc.vector.memset(f_plane_raw[:].rearrange("p g c -> p (g c)").bitcast(I32), 0)
        nc.vector.memset(p_plane[:].rearrange("p h c -> p (h c)").bitcast(I32), 0)
        ident_bf = kept("ident_bf", [P, P], BF16)
        nc.vector.tensor_copy(out=ident_bf[:], in_=ident[:])

        x_codes = [kept("x_codes%d" % g, [P, B], U32) for g in range(3)]
        x_plane = [kept("x_plane%d" % g, [P, B], U8) for g in range(3)]
        v_codes = [kept("v_codes%d" % h, [P, B], U32) for h in range(2)]
        v_plane = [kept("v_plane%d" % h, [P, B], U8) for h in range(2)]
        y_codes = kept("y_codes", [P, 2, B], U32)
        y_plane = kept("y_plane", [P, 2, B], U8)

        logs, z_pair, sorted_words, flow, expo, y_f32, y_bf = {}, {}, {}, {}, {}, {}, {}
        f_raw, f_codes, f_plane, e_raw, e_slots, e_codes, e_plane = {}, {}, {}, {}, {}, {}, {}

        def load_first_chunk(g):
            source = log_x[:GROUP, GROUP * g : GROUP * (g + 1)] if g < 2 else log_z[:GROUP, :]
            four = kept("first%d" % g, [P, CHUNK, GROUP], BF16)
            nc.sync.dma_start(out=four[:], in_=source.rearrange("(j p) k -> p j k", j=CHUNK))
            for j in range(CHUNK):
                logs[j, g] = four[:, j, :]

        def load_pair(a):
            for j in (a, a + 1):
                x_tile = staged("x_tile", [P, S], BF16, 8)
                nc.sync.dma_start(out=x_tile[:], in_=log_x[j * P : (j + 1) * P, :])
                logs[j, 0], logs[j, 1] = x_tile[:, :GROUP], x_tile[:, GROUP:]
            z_pair[a] = staged("z_pair", [P, 2, Z], BF16, 4)
            nc.sync.dma_start(out=z_pair[a][:], in_=log_z[a * P : (a + 2) * P, :].rearrange("(j p) k -> p j k", j=2))
            logs[a, 2], logs[a + 1, 2] = z_pair[a][:, 0, :], z_pair[a][:, 1, :]

        def load_flow(j):
            flow[j] = staged("flow", [P, S], BF16, 5)
            nc.sync.dma_start(out=flow[j][:], in_=inflow[j * P : (j + 1) * P, :])

        def load_planes(plane, scale_rows):
            for q in range(4):
                nc.sync.dma_start(
                    out=plane[32 * q : 32 * q + 4, :, :].bitcast(I32),
                    in_=scale_rows[:, 4 * q : 4 * q + 4, :].rearrange("g r c -> r g c").bitcast(I32),
                )

        def load_f(h):
            f_raw[h] = kept("f_raw%d" % h, [P, 2, 2 * GROUP], U8)
            nc.sync.dma_start(
                out=f_raw[h][:].bitcast(I32),
                in_=f_words[:, :, 2 * GROUP * h : 2 * GROUP * (h + 1)].rearrange("g p b -> p g b").bitcast(I32),
            )

        def load_e(h):
            e_raw[h] = wide_tile([P, 4, GROUP], BF16)
            nc.sync.dma_start(
                out=e_raw[h][:], in_=e_orders[:, GROUP * h : GROUP * (h + 1)].rearrange("(p s) c -> p s c", s=4)
            )

        def sort_f_codes(h):
            f_codes[h] = kept("f_codes%d" % h, [P, 2, 2 * GROUP], U8)
            nc.vector.tensor_copy(
                out=f_codes[h][:].rearrange("p g (t m b) -> p g t m b", t=4, b=2),
                in_=f_raw[h][:].rearrange("p g (m t b) -> p g t m b", t=4, b=2),
            )

        def sort_f_plane(h):
            f_plane[h] = kept("f_plane%d" % h, [P, 2, GROUP], U8)
            nc.vector.tensor_copy(
                out=f_plane[h][:].rearrange("p g (t m) -> p g t m", t=4),
                in_=f_plane_raw[:, :, GROUP * h : GROUP * (h + 1)].rearrange("p g (m t) -> p g t m", t=4),
            )

        def sort_e(h):
            e_slots[h] = wide_tile([P, 4 * GROUP], BF16)
            nc.vector.tensor_copy(
                out=e_slots[h][:].rearrange("p (t a b s) -> p a t b s", t=4, b=2, s=4),
                in_=e_raw[h][:].rearrange("p s (a b t) -> p a t b s", b=2, t=4),
            )

        def quantise_e(h):
            e_codes[h] = kept("e_codes%d" % h, [P, GROUP], U32)
            e_plane[h] = kept("e_plane%d" % h, [P, GROUP], U8)
            nc.vector.quantize_mx(out=e_codes[h][:].bitcast(FP8X4), scales=e_plane[h][:], in_=e_slots[h][:])

        consts = psum.tile([P, 2 * GROUP], BF16, name="consts", tag="consts")
        unit_high = consts[:, GROUP:]
        unit_down = kept("unit_down", [P, 4, 2], BF16)
        unit_low = kept("unit_low", [P, POOL_COLS], BF16)

        def turn_constants_down():
            for t in range(4):
                nc.tensor.transpose(consts[:, t * P : (t + 1) * P], const_rows[:, t:GROUP:4], ident_bf[:])
            bank = turn_bank()[:].bitcast(BF16)
            for c in range(4):
                nc.tensor.transpose(bank[:, c * P : (c + 1) * P], const_rows[:, c * P : (c + 1) * P], ident_bf[:])
            nc.scalar.copy(out=unit_down[:], in_=bank[:, :GROUP].rearrange("p (c r) -> p c r", c=4)[:, :, 2:4])

        def spread_unit():
            bank = turn_bank()[:].bitcast(BF16)
            for c in range(POOL_COLS // P):
                column = unit_down[:, c % 4, c // 4 : c // 4 + 1]
                nc.tensor.transpose(bank[:, c * P : (c + 1) * P], column.to_broadcast([P, P]), ident_bf[:])
            for c in range(4):
                column = unit_down[:, c, 1:2]
                nc.tensor.transpose(unit_high[:, c * P : (c + 1) * P], column.to_broadcast([P, P]), ident_bf[:])
            nc.scalar.copy(out=unit_low[:], in_=bank[:, :POOL_COLS])

        def quantise(slots, codes, plane, a, b):
            nc.vector.quantize_mx(
                out=codes[:, a * P : b * P].bitcast(FP8X4), scales=plane[:, a * P : b * P], in_=slots[:, : (b - a) * GROUP]
            )

        def turn(words_of, a, b, copy):
            count = b - a
            bank = turn_bank()
            for j in range(a, b):
                for u in range(2):
                    place = 2 * (j - a) + u
                    nc.tensor.transpose(bank[:, place * P : (place + 1) * P], words_of(j, u), ident[:])
            slots = slot_tile()
            copy(
                out=slots[:, : count * GROUP].bitcast(F32).rearrange("p (j c u) -> p j c u", j=count, u=2),
                in_=bank[:, : count * 2 * P].rearrange("p (j u c) -> p j c u", j=count, u=2),
            )
            return slots

        def sort_words(a):
            for g in range(3):
                words = staged("words", [P, 2, 2 * P], F32, 6)
                if g < 2:
                    for j in range(2):
                        nc.vector.tensor_copy(
                            out=words[:, j, :].rearrange("p (u c r) -> p c u r", u=2, r=4),
                            in_=logs[a + j, g].bitcast(F32).rearrange("p (c r u) -> p c u r", u=2, r=4),
                        )
                else:
                    nc.vector.tensor_copy(
                        out=words[:].rearrange("p j (u c r) -> p j c u r", u=2, r=4),
                        in_=z_pair[a][:].bitcast(F32).rearrange("p j (c r u) -> p j c u r", u=2, r=4),
                    )
                sorted_words[a, g] = words

        def turn_in(a, g):
            if a in SORTED_PAIRS:
                slots = turn(lambda j, u: sorted_words[a, g][:, j - a, u * P : (u + 1) * P], a, a + 2, nc.scalar.copy)
            else:
                slots = turn(lambda j, u: logs[j, g].bitcast(F32)[:, u : 2 * P : 2], a, a + 2, nc.scalar.copy)
            return lambda: quantise(slots, x_codes[g], x_plane[g], a, a + 2)

        def turn_in_pair(a):
            return [turn_in(a, g) for g in range(3)]

        def turn_out(a, b, n, copy=nc.scalar.copy):
            slots = turn(lambda j, u: y_bf[j][:].bitcast(F32)[:, (2 * n + u) * P : (2 * n + u + 1) * P], a, b, copy)
            return lambda: quantise(slots, y_codes[:, n, :], y_plane[:, n, :], a, b)

        def turn_out_pair(a):
            return [turn_out(a, a + 2, n) for n in range(2)]

        def exponent_pass(bank, a, h, t, g):
            cells = slice(a * P, (a + CHUNK) * P)
            if g < 2:
                orders = f_codes[h][:, g, 2 * P * t : 2 * P * (t + 1)].bitcast(FP4X4)
                orders_plane = f_plane[h][:, g, P * t : P * (t + 1)]
            else:
                orders = e_codes[h][:, P * t : P * (t + 1)].bitcast(FP8X4)
                orders_plane = e_plane[h][:, P * t : P * (t + 1)]
            nc.tensor.matmul_mx(
                out=bank[:], lhsT=orders, lhsT_scale=orders_plane,
                rhs=x_codes[g][:, cells].bitcast(FP8X4), rhs_scale=x_plane[g][:, cells],
                start=(g == 0), stop=(g == 2),
            )

        def exponential(bank, a, h, t):
            if t == 0:
                expo[a, h] = staged("expo", [P, 4, GROUP], F32, 3)
            nc.scalar.activation(out=expo[a, h][:, t, :], in_=bank[:], func=ACT.Exp)

        def stage1(a, h, t):
            bank = sum_bank()
            for g in range(3):
                exponent_pass(bank, a, h, t, g)
            exponential(bank, a, h, t)

        def rates(a, h):
            first = a - a % CHUNK
            cells = slice((a - first) * P, (a - first + 2) * P)
            rate = consts[:, :GROUP].rearrange("p (t r) -> p t r", t=4)[:, :, h]
            slots = slot_tile()
            nc.vector.tensor_tensor(
                out=slots[:].rearrange("p (c i t) -> p c t i", i=2, t=4),
                in0=expo[first, h][:, :, cells].rearrange("p t (c i) -> p c t i", i=2),
                in1=rate.unsqueeze(1).unsqueeze(3).to_broadcast([P, P, 4, 2]),
                op=ALU.mult,
            )
            return lambda: quantise(slots, v_codes[h], v_plane[h], a, a + 2)

        def pool_cols(j):
            return POOL_COLS if j <= LAST_STEP else GROUP

        def stage2_half(j, n):
            if n == 0:
                y_f32[j] = wide_tile([P, S], F32)
            cells = slice(j * P, (j + 1) * P)
            cols = slice(GROUP * n, GROUP * (n + 1))
            bank = sum_bank()
            for h in range(2):
                nc.tensor.matmul_mx(
                    out=bank[:], lhsT=v_codes[h][:, cells].bitcast(FP8X4), lhsT_scale=v_plane[h][:, cells],
                    rhs=p_codes[:, h, cols].bitcast(FP8X4), rhs_scale=p_plane[:, h, cols],
                    start=(h == 0), stop=(h == 1),
                )
            nc.vector.tensor_tensor(out=y_f32[j][:, cols], in0=bank[:], in1=flow[j][:, cols], op=ALU.add)
            share = slice(GROUP * n, min(GROUP * (n + 1), pool_cols(j)))
            if share.stop > share.start:
                nc.gpsimd.tensor_tensor(out=y_f32[j][:, share], in0=y_f32[j][:, share], in1=unit_low[:, share], op=ALU.mult)

        def stage2(j):
            stage2_half(j, 0)
            stage2_half(j, 1)

        def to_mass(j):
            c = pool_cols(j)
            nc.vector.tensor_tensor(out=y_f32[j][:, c:], in0=y_f32[j][:, c:], in1=unit_high[:, c - GROUP :], op=ALU.mult)

        def new_y_bf(j):
            y_bf[j] = staged("y_bf", [P, S], BF16, 4)

        def store_and_round(j):
            nc.sync.dma_start(out=out_0[j * P : (j + 1) * P, :], in_=y_f32[j][:])
            new_y_bf(j)
            nc.scalar.copy(
                out=y_bf[j][:].rearrange("p (n u q e) -> p n u q e", n=2, u=2, e=2),
                in_=y_f32[j][:].rearrange("p (n q u e) -> p n u q e", n=2, u=2, e=2),
            )

        def store_and_round_half(j, n, copy):
            cols = slice(GROUP * n, GROUP * (n + 1))
            nc.sync.dma_start(out=out_0[j * P : (j + 1) * P, cols], in_=y_f32[j][:, cols])
            copy(
                out=y_bf[j][:, cols].rearrange("p (u q e) -> p u q e", u=2, e=2),
                in_=y_f32[j][:, cols].rearrange("p (q u e) -> p u q e", u=2, e=2),
            )

        def store_codes(a, b, queue=nc.sync):
            queue.dma_start(
                out=out_1[:, :, a * P : b * P, :].rearrange("n p c t -> p n (c t)").bitcast(I32),
                in_=y_codes[:, :, a * P : b * P].bitcast(I32),
            )

        def store_planes(a, b):
            for q in range(4):
                nc.sync.dma_start(
                    out=out_2[:, 4 * q : 4 * q + 4, a * P : b * P].rearrange("n r c -> r n c").bitcast(I32),
                    in_=y_plane[32 * q : 32 * q + 4, :, a * P : b * P].bitcast(I32),
                )

        load_first_chunk(0)
        load_f(0)
        load_first_chunk(1)
        load_planes(f_plane_raw, f_scales)
        nc.sync.dma_start(out=const_rows[0:2, :], in_=rate_const.rearrange("(h c) -> h c", h=2))
        nc.sync.dma_start(out=const_rows[2:4, :], in_=unit.rearrange("(n c) -> n c", n=2))
        load_first_chunk(2)
        load_e(0)
        load_f(1)
        load_e(1)
        load_pair(4)
        load_pair(6)
        p_codes = kept("p_codes", [P, 2, S], U32)
        nc.sync.dma_start(out=p_codes[:].bitcast(I32), in_=p_words.rearrange("h p c t -> p h (c t)").bitcast(I32))
        load_planes(p_plane, p_scales)
        load_flow(0)
        load_flow(1)

        quantise_x = [turn_in(0, 0), turn_in(2, 0)]
        sort_f_codes(0)
        run(quantise_x)
        quantise_x = [turn_in(0, 1), turn_in(2, 1)]
        sort_f_plane(0)
        turn_constants_down()
        run(quantise_x)
        sort_f_plane(1)
        banks = [sum_bank() for t in range(4)]
        for t in (0, 1):
            exponent_pass(banks[t], 0, 0, t, 0)
        quantise_x = [turn_in(0, 2), turn_in(2, 2)]
        sort_e(0)
        for t in (2, 3):
            exponent_pass(banks[t], 0, 0, t, 0)
        for t in range(4):
            exponent_pass(banks[t], 0, 0, t, 1)
        quantise_e(0)
        run(quantise_x)
        sort_f_codes(1)
        sort_e(1)
        for t in range(4):
            exponent_pass(banks[t], 0, 0, t, 2)
            exponential(banks[t], 0, 0, t)
        quantise_e(1)

        quantise_x = turn_in_pair(4)
        quantise_v = rates(0, 0)
        stage1(0, 1, 0)
        stage1(0, 1, 1)
        run(quantise_x + [quantise_v])
        quantise_v = rates(2, 0)
        quantise_x = turn_in_pair(6)
        stage1(0, 1, 2)
        stage1(0, 1, 3)
        run(quantise_x + [quantise_v])

        waiting = []
        for k in range(-1, LAST_STEP + 1):
            if k + 2 in TURN_IN_STEP:
                load_pair(TURN_IN_STEP[k + 2])
            load_flow(k + 3)
            run(waiting)
            waiting = []
            if TURN_IN_STEP.get(k + 1) in SORTED_PAIRS:
                sort_words(TURN_IN_STEP[k + 1])
            if k == 0:
                spread_unit()
            if k in TURN_IN_STEP:
                waiting.extend(turn_in_pair(TURN_IN_STEP[k]))
            if k >= 3 and k % 2 == 1:
                waiting.extend(turn_out_pair(k - 3))
                if (k - 1) % CHUNK == 0:
                    waiting.append(lambda end=k - 1: store_codes(end - CHUNK, end))
            if k >= 1:
                store_and_round(k - 1)
            if k >= 0:
                stage2(k)
            chunk, piece = divmod(k + RATE_LEAD, CHUNK)
            waiting.insert(1, rates(CHUNK * chunk + 2 * (piece % 2), piece // 2))
            if k >= 0:
                to_mass(k)
            chunk, piece = divmod(k + STAGE1_LEAD, CHUNK)
            for t in (2 * (piece % 2), 2 * (piece % 2) + 1):
                stage1(CHUNK * chunk, piece // 2, t)

        load_flow(14)
        run(waiting)
        quantise_y = turn_out_pair(8)
        quantise_v = rates(12, 1)
        store_and_round(10)
        load_flow(15)
        run([quantise_y[0], quantise_v, quantise_y[1]])
        store_codes(8, 10)
        store_planes(0, 10)
        stage2(11)
        stage2_half(12, 0)
        to_mass(11)
        store_and_round(11)
        stage2_half(12, 1)
        quantise_v = rates(14, 1)
        to_mass(12)
        quantise_v()
        stage2(13)
        quantise_y = turn_out_pair(10)
        store_and_round(12)
        for j in (13, 14):
            stage2_half(j + 1, 0)
            to_mass(j)
            store_and_round(j)
            stage2_half(j + 1, 1)
        quantise_y[0]()
        to_mass(15)
        quantise_y[1]()
        store_codes(10, 12)

        quantise_y = turn_out_pair(12)
        new_y_bf(15)
        store_and_round_half(15, 0, nc.vector.tensor_copy)
        quantise_14 = [turn_out(14, 15, n, nc.vector.tensor_copy) for n in range(2)]
        store_and_round_half(15, 1, nc.scalar.copy)
        run(quantise_y)
        store_codes(12, 14)
        quantise_15 = [turn_out(15, 16, 0, nc.vector.tensor_copy), turn_out(15, 16, 1)]
        run(quantise_14 + quantise_15)
        store_codes(14, 16, nc.scalar)
        store_planes(10, 16)
